import numpy as np, ml_dtypes
CORES = [5,29,101,125,133,157,229,253]
N = 8
BF = ml_dtypes.bfloat16
W, K, E, TH, ST, RO = 4096, 256, 16, 10, 1, 5
def subset(rng, cnt):
    a = 2 * rng.integers(0, 8, cnt.shape) + 1; o = rng.integers(0, 16, cnt.shape)
    return (((a * np.arange(16)[:, None] + o) & 15) < cnt).astype(np.int16)
def parts(rng):
    x = rng.integers(0, 256, (N, 8, 1, W), dtype=np.int16) + rng.integers(-12, 13, (N, 8, 16, W), dtype=np.int16)
    x = np.where(rng.random((N, 8, 1, W)) < 0.125, rng.integers(0, 256, (N, 8, 16, W), dtype=np.int16), np.clip(x, 0, 255))
    stk = rng.integers(0, W, (N, 8, 16, K)); bas = rng.integers(0, W, (N, 8, 16, K)); con = rng.integers(0, W, (N, 8, 16, K)); ln = rng.integers(1, 16, (N, 8, K))
    lv = (255.0 * (1.0 - rng.random((N, 8, 1, K)) ** 2)).astype(np.int64)
    z = np.clip(lv + rng.integers(-12, 13, (N, 8, 16, K)), 0, 255); w = rng.integers(1, 258, (N, 8, 16, 1))
    return x, stk, bas, con, ln, z, w
def pack(x, stk, bas, con, ln, z, w):
    def t(a, n): return np.ascontiguousarray(np.reshape(a, (N, 128, n)))
    return {"xt": t(x, W).astype(np.float32).astype(BF), "stk": t(stk, K).astype(np.int32), "bas": t(bas, K).astype(np.int32), "con": t(con, K).astype(np.int32),
            "ln": np.ascontiguousarray(ln).astype(np.int32), "z": t(z, K).astype(np.float32).astype(BF), "w": t(w, 1).astype(np.int32)}
def setup_inputs(rng):
    return pack(*parts(rng))
def setup_inputs_spread(rng):
    x, stk, bas, con, ln, z, w = parts(rng)
    x = (np.exp2(8.0 * rng.random((N, 8, 1, W), dtype=np.float32)) * rng.random((N, 8, 16, W), dtype=np.float32)).astype(np.int16)
    x = np.minimum(x, 255) * (rng.random((N, 8, 1, W)) > 0.0625)
    z = np.minimum((np.exp2(8.0 * rng.random((N, 8, 1, K))) * rng.random((N, 8, 16, K))).astype(np.int64), 255)
    def skew(lo, n, shape):
        e = rng.choice(np.array([0.25, 1.0, 4.0]), (N, 8) + (1,) * (len(shape) - 2))
        return np.minimum(lo + (n * rng.random(shape) ** e).astype(np.int64), lo + n - 1)
    stk = skew(0, W, (N, 8, 16, K)); bas = skew(0, W, (N, 8, 16, K)); con = skew(0, W, (N, 8, 16, K)); ln = skew(1, 15, (N, 8, K))
    w = np.minimum(np.exp2(8.01 * rng.random((N, 8, 16, 1))).astype(np.int64), 257)
    return pack(x, stk, bas, con, ln, z, w)
def endnames(rng):
    a = (W - 1) * rng.integers(0, 2, (N, 8, 16, K))
    s = (W - 1) * ((np.arange(16)[:, None] >= rng.integers(0, 17, (N, 8, 1, K))).astype(np.int64) ^ rng.integers(0, 2, (N, 8, 1, K)))
    ty = rng.random((N, 8, 1, K))
    return np.where(ty < 0.4, a, np.where(ty < 0.75, s, rng.integers(0, W, (N, 8, 16, K))))
def setup_inputs_ends(rng):
    cnt = rng.choice(np.array([0, 1, TH - 2, TH - 1, TH, 12, 16]), (N, 8, 1, W)); cnt[1] = np.minimum(cnt[1], TH - 2)
    x = 255 * subset(rng, cnt)
    zc = rng.choice(np.array([0, 1, 3, TH - 1, TH, 12]), (N, 8, 1, K)); zc[0] = rng.choice(np.array([TH, 12, 15]), (8, 1, K)); zc[1] = 1
    z = 255 * (1 - subset(rng, zc)); stk = endnames(rng); bas = endnames(rng); con = endnames(rng)
    for k in (0, K // 2, K - 1): z[1, 0, :, k] = 0
    ln = 1 + 14 * rng.integers(0, 2, (N, 8, K)); w = 1 + 256 * rng.integers(0, 2, (N, 8, 16, 1)); q = N - 1
    w[q, 7] = 257; w[q, 0] = 1; w[q, 6, 0] = 257; x[q, 6:8, :, 0] = 0; x[q, 7, :, W - 1] = 255; x[q, 6, :, W - 1] = 0; x[q, 6, 0, W - 1] = 255
    for k in (0, K - 1): stk[q, 7, :, k] = 0; stk[q, 7, 15, k] = W - 1
    for k in (1, K - 2): stk[q, 7, :, k] = W - 1
    for k in (2, K - 3): stk[q, 7, :, k] = 0; stk[q, 7, 0, k] = W - 1
    for k in (0, 1, 2, K - 3, K - 2, K - 1): z[q, 7, :, k] = 255
    for k in (2, K - 1): stk[q, 6, :, k] = W - 1; z[q, 6, :12, k] = 0; z[q, 6, 12:, k] = 255
    return pack(x, stk, bas, con, ln, z, w)
def setup_inputs_corners(rng):
    x, stk, bas, con, ln, z, w = parts(rng)
    cnt = rng.choice(np.array([0, TH - 1, TH, 16]), (N, 8, 1, W))
    over = rng.integers(0, 2, (N, 8, 1, W), dtype=np.int16) * rng.integers(0, 56, (N, 8, 16, W), dtype=np.int16)
    x = np.where(subset(rng, cnt) > 0, 200 + over, rng.integers(0, 200, (N, 8, 16, W), dtype=np.int16))
    z[:] = np.where(rng.random((N, 8, 1, K)) < 0.125, 201, 200); i = np.arange(16)[:, None]
    for q in range(N):
        for g in range(8):
            hot = np.flatnonzero(cnt[q, g, 0] >= TH); cold = np.flatnonzero(cnt[q, g, 0] < TH)
            row = rng.integers(1, 17, K); row[0] = 1; row[1] = 16; row[2] = 14; row[K - 1] = 15; row[K - 2] = 16
            hn = hot[rng.integers(0, len(hot), (16, K))]; cn = cold[rng.integers(0, len(cold), (16, K))]
            stk[q, g] = np.where(i == row, hn, np.where(i > row, stk[q, g], np.where((i == 0) & (rng.random((1, K)) < 0.5), hn, cn)))
    ln = rng.choice(np.array([1, 2, 14, 15]), (N, 8, K))
    for q in range(N): ln[q, q % 8] = 15; ln[q, (q + 1) % 8] = 1
    four = np.arange(K) % 4; stk[:, 3] = stk[:, 3][..., four]; z[:, 3] = z[:, 3][..., four]
    bas[:, 4] = (W - 1) * rng.integers(0, 2, (N, 16, K)); con[:, 2] = (W - 1) * rng.integers(0, 2, (N, 16, K))
    stk[:, 5] = stk[:, 5, :1].copy(); stk[:, 6] = E * np.arange(K) + rng.integers(0, E, (N, 16, K)); bas[:, 6] = E * np.arange(K) + rng.integers(0, E, (N, 16, K))
    w[0] = 1; w[N - 1] = 257
    return pack(x, stk, bas, con, ln, z, w)
def setup_inputs_long(rng):
    x, stk, bas, con, ln, z, w = parts(rng)
    x = np.where(rng.random((N, 8, 1, W)) < 0.06, rng.integers(250, 254, (N, 8, 16, W), dtype=np.int16), np.minimum(x, 249))
    ty = rng.random((N, 8, 1, K)); z = np.where(ty < 0.4, 250, np.where(ty < 0.8, 254, z)); ln = np.maximum(ln, rng.integers(1, 16, (N, 8, K)))
    return pack(x, stk, bas, con, ln, z, w)
def setup_inputs_alike(rng):
    x, stk, bas, con, ln, z, w = parts(rng); ga, gb, gc = [int(g) for g in rng.permutation(8)[:3]]; o = int(rng.integers(0, N))
    for a in (stk, bas, con):
        a[:, gb] = np.where(rng.random((N, 16, K)) < 0.5, E * rng.integers(K - 16, K, (N, 16, K)) + E - 1, a[:, gb])
    w[:, gb] = E * rng.integers(1, 256 // E + 1, (N, 16, 1)); w[:, gb, 0] = 1 + 256 * rng.integers(0, 2, (N, 1))
    for i in range(N):
        q = (o + i * ST) % N; lo, hi = ((32, 63), (96, 127), (192, 254), (96, 127), (0, 255))[min(i, 4)]
        if i < 4:
            x[q] = rng.integers(lo, hi + 1, (8, 16, W)); z[q] = 255 if i == 1 else 0
        if i == 2:
            m = np.zeros(8 * K, dtype=bool); m[rng.permutation(8 * K)[:K * int(rng.integers(0, 8)) + int(rng.integers(1, K))]] = True
            z[q] = np.where(m.reshape(8, 1, K), 255, 0)
        for g, v in ((ga, int(rng.integers(1, 4))), (gc, 0)):
            one = rng.integers(lo, hi - 2, 16); one[15] += (v - int(np.sum(one))) % 4
            x[q, g] = one[:, None]
        x[q, gb, 0] = (hi + 1) // E * E - 1
    return pack(x, stk, bas, con, ln, z, w)
def check_inputs(d):
    bad = []
    for k, lo, hi in (("xt", 0, 255), ("stk", 0, W - 1), ("bas", 0, W - 1), ("con", 0, W - 1), ("ln", 1, 15), ("z", 0, 255), ("w", 1, 257)):
        v = np.asarray(d[k]).astype(np.float32)
        if not (np.min(v) >= lo and np.max(v) <= hi and np.all(v == np.floor(v))): bad.append("range of " + k)
    return bad
def reference(xt, stk, bas, con, ln, z, w):
    X = xt.astype(np.float32).astype(np.int32).reshape(N, 8, 16, W); Z = z.astype(np.float32).astype(np.int64).reshape(N, 8, 16, K); wt = w.astype(np.int64).reshape(N, 8, 16, 1)
    S = stk.astype(np.int64).reshape(N, 8, 16, K); B = bas.astype(np.int64).reshape(N, 8, 16, K); C = con.astype(np.int64).reshape(N, 8, 16, K); n = ln.astype(np.int64).reshape(N, 8, K)
    A = [0] * N; p = np.arange(16)[None, :, None]
    for t in range(RO):
        for q in range(N):
            b = (q - t * ST) % N
            s, zz = S[b].copy(), Z[b].copy()
            R = np.take_along_axis(X[q], s.reshape(8, 1, 16 * K), 2).reshape(8, 16, 16, K).astype(np.int64)
            votes = np.add.reduce((R >= zz[:, :, None, :]).astype(np.int64), axis=1)
            hit = votes >= TH; hit[:, 0] = False
            found = np.maximum.accumulate(hit.astype(np.int64), axis=1)
            handled = found[:, 15] == 1; h = 16 - np.add.reduce(found, axis=1)
            M = np.max(np.where(found[:, None] == 1, 0, R), axis=2)
            u = np.add.reduce(wt[q] * M, axis=1) & 4095
            xh = np.take_along_axis(R, np.minimum(h, 15)[:, None, None, :], 2)[:, :, 0]
            v = np.add.reduce(xh, axis=1) & 3
            j = (((u * u) >> 5) + u + A[q]) & (K - 1)
            paste = handled & (v > 0)
            m = np.where(paste, np.take_along_axis(n[q], j, 1), 0)
            src = p + (np.where(paste, h + 1, h) - m)[:, None, :]
            low = np.take_along_axis(s, np.clip(src, 0, 15), 1); piece = np.take_along_axis(C[q], j[:, None, :], 2)
            new = np.where(p < m[:, None, :], piece, np.where(src <= 15, low, B[b]))
            S[b] = np.where(handled[:, None, :], new, s)
            Z[b] = np.where(handled[:, None, :], np.abs(xh - zz), M)
            C[q] = np.where(paste[:, None, :] & (p < h[:, None, :]), s, C[q])
            n[q] = np.where(paste, h, n[q])
            A[q] = int(np.sum(np.where(handled, 0, 1)))
            if t < RO - 1:
                col = (E * np.arange(K) + (u & (E - 1)))[:, None, :]
                np.put_along_axis(X[q], col, ((np.take_along_axis(X[q], col, 2) + M) >> 1).astype(np.int32), 2)
    last = [(q - (RO - 1) * ST) % N for q in range(N)]
    return {"ys": S[last].reshape(N, 128, K).astype(np.float32), "yc": C.reshape(N, 128, K).astype(np.float32), "yn": n.astype(np.float32), "yz": Z[last].reshape(N, 128, K).astype(np.float32).astype(BF)}

@@ -1,0 +1,663 @@
+from concourse.bass import DstId, RemoteDMATransfer
+from concourse.mybir import dt, AluOpType as A, AxisListType, ActivationFunctionType as F
+
+NT = 5
+K = 256
+NC = 2
+n = K // NC
+VR = 7
+GSPLIT = (("V", 0, 64), ("S", 64, 128))
+LAT = 5000
+HV = (1, 1)
+LEV = "ABCDEFGHIJKLMNOPQRSTUVWXYZabcdefghijklmnopqrstuvwxyz0123456789+-"
+BTS = "Oo0QdjyyhW1pc1f-lxmQhgihFAjggew-SI0d1spaomGwWOZond35Axiz38ozCijsFKvg-jznb+qk-lqv7gbdZNpd6cGrhqyav7nf5e-3nNTzpsUdspvcbdcpdowVRQP3OeVlZ3jV-06hcaf3mcrffcwveehl8eW"
+PEC = 0.5
+SX = 80
+WS = 45
+RWN = 4
+WK = 100
+BONUS = 6000.0
+SLK = 60
+CD = 264
+W1 = n // 16
+RW = 16 * n
+
+SCRATCH = {
+    "tab": ("sbuf", [128, 4096], "bfloat16"),
+    "stl": ("sbuf", [128, NT * K], "uint16"), "sto": ("sbuf", [128, NT * K], "uint16"),
+    "zl": ("sbuf", [128, NT * K], "bfloat16"), "zo": ("sbuf", [128, NT * K], "bfloat16"),
+    "bl": ("sbuf", [128, NT * K], "float16"),
+    "stkI": ("sbuf", [128, K], "int32"), "basI": ("sbuf", [128, K], "int32"), "conI": ("sbuf", [128, K], "int32"),
+    "lnI": ("sbuf", [8, K], "int32"), "lnB": ("sbuf", [8, K], "bfloat16"), "wI": ("sbuf", [128, 1], "int32"),
+    "stf": ("sbuf", [128, K], "float32"),
+    "S": ("sbuf", [128, 16 * 128], "bfloat16"), "Wm": ("sbuf", [128, 16 * 128], "float16"),
+    "Rot": ("sbuf", [128, 16 * 128], "float16"),
+    "cm": ("sbuf", [128, 12 * 128], "bfloat16"),
+    "I2k": ("sbuf", [128, 128], "float16"),
+    "E8": ("sbuf", [8, 128], "bfloat16"), "E8i": ("sbuf", [8, 128], "int32"),
+    "ib": ("sbuf", [128, 4 * 128], "int32"), "fb": ("sbuf", [128, 3 * 128], "float32"),
+    "ki": ("sbuf", [128, 16], "int32"), "kf": ("sbuf", [128, 64], "float32"), "kb": ("sbuf", [128, 64], "bfloat16"),
+    "pi": ("sbuf", [128, 2], "int32"), "pf": ("sbuf", [128, 16], "float32"),
+    "smask": ("sbuf", [128, RW], "bfloat16"), "cst": ("sbuf", [128, NT * n], "float16"),
+    "AW": ("sbuf", [128, CD + K], "float32"), "asel": ("sbuf", [128, K], "float32"),
+    "CW0": ("sbuf", [128, CD + K], "float32"), "CW1": ("sbuf", [128, CD + K], "float32"),
+    "YW0": ("sbuf", [128, CD + K], "bfloat16"), "YW1": ("sbuf", [128, CD + K], "bfloat16"),
+    "lm0": ("sbuf", [128, K], "float32"), "sel": ("sbuf", [128, 16], "uint16"), "unb": ("sbuf", [128, 16], "bfloat16"),
+    "ac": ("sbuf", [128, 8], "float32"), "ai": ("sbuf", [128, 8], "int32"),
+    "yci": ("sbuf", [128, K], "int32"), "ycj": ("sbuf", [128, K], "int32"), "ycf": ("sbuf", [128, K], "float32"), "ynf": ("sbuf", [8, K], "float32"),
+    "pz": ("psum", [128, 512], "float32"),
+}
+for _c in range(NC):
+    for _nm, _w, _d in (("R", RW + 16, "bfloat16"), ("P", RW + 16, "bfloat16"), ("GE", RW, "bfloat16"),
+                        ("hit", n, "bfloat16"), ("nf", n, "bfloat16"), ("AM", 2 * n, "bfloat16"), ("xh", n, "bfloat16"),
+                        ("sb", n, "float16"), ("rotW", RW, "float32"), ("rg", n, "float32"), ("pm", n, "float16"),
+                        ("yg", n, "bfloat16"), ("nmp", n, "float16"), ("rotK", n, "float16"),
+                        ("baM", n, "float16"), ("wi", 16 * W1, "int32"), ("wf", 16 * W1, "float32"),
+                        ("wl", 8 * W1, "uint16"), ("pvb", W1, "bfloat16"), ("told", n, "int32"), ("tnew", n, "int32")):
+        SCRATCH[_nm + "c%d" % _c] = ("sbuf", [128, _w], _d)
+    SCRATCH["pa%d" % _c] = ("psum", [128, 512], "float32")
+    SCRATCH["pw%d" % _c] = ("psum", [128, 512], "float32")
+for _x in range(3):
+    SCRATCH["pd%d" % _x] = ("psum", [128, 512], "float32")
+
+LOADS = ["xt", "stk", "z", "w", "ln", "con", "bas"]
+SEMAPHORES = (["sV", "sS", "sP", "sG", "lo", "outs"] + ["ld_" + x for x in LOADS]
+              + ["%s%d_%d" % (p, t, c) for p in ("s", "z", "b") for t in range(1, NT) for c in range(NC)]
+              + ["h%s%d_%d" % (p, t, c) for p in ("s", "z") for t in range(1, NT) for c in range(NC)]
+              + ["hb%d" % t for t in range(NT)])
+
+CY = 0.83 * 1.2
+
+
+def vc(m, f=1.0):
+    return CY * max(64, m * f) + 15
+
+
+def gc_(m):
+    return 60 + 1.5 * CY * m
+
+
+def pc(*ms):
+    return sum(PEC * max(64, m) for m in ms)
+
+
+ORDERS = {}
+
+
+def schedule(nodes):
+    N = len(nodes)
+    succ = [[] for _ in range(N)]
+    for i, x in enumerate(nodes):
+        for d in x["deps"]:
+            succ[d].append(i)
+    pri = [0.0] * N
+    for i in range(N - 1, -1, -1):
+        pri[i] = nodes[i]["cost"] + 60 + max([pri[j] for j in succ[i]] + [0.0])
+    for i in range(N):
+        pri[i] += nodes[i]["bonus"]
+    left = [len(x["deps"]) for x in nodes]
+    ready = {}
+    est = [0.0] * N
+    for i in range(N):
+        if left[i] == 0:
+            ready.setdefault(nodes[i]["eng"], set()).add(i)
+    free = {}
+    opened = set()
+    bank = {}
+    order, extra = [], [()] * N
+    end = [0.0] * N
+    while len(order) < N:
+        best = None
+        for e, rs in ready.items():
+            if not rs:
+                continue
+            f = free.get(e, 0.0)
+            c = []
+            for i in rs:
+                if e == "P" and nodes[i]["grp"] < 2 and opened & set(nodes[i]["banks"]):
+                    continue
+                s = max(est[i], f if e != "net" else 0.0)
+                for b in nodes[i]["banks"]:
+                    lb = bank.get(b)
+                    if lb and nodes[lb]["eng"] != e:
+                        s = max(s, end[lb] + 60)
+                c.append((s, i))
+            if not c:
+                continue
+            m = min(c)[0]
+            k = max((pri[i], -s, i) for s, i in c if s <= m + SLK)
+            if best is None or m < best[0]:
+                best = (m, k[2], -k[1])
+        i, s = best[1], best[2]
+        x = nodes[i]
+        e = x["eng"]
+        ready[e].discard(i)
+        end[i] = s + x["cost"]
+        free[e] = end[i]
+        ex = []
+        for b in x["banks"]:
+            lb = bank.get(b)
+            if lb is not None and nodes[lb]["eng"] != e:
+                ex.append(lb)
+            bank[b] = i
+        extra[i] = tuple(ex)
+        if x["grp"] == 1:
+            opened.update(x["banks"])
+        elif x["grp"] == 3:
+            opened.difference_update(x["banks"])
+        order.append(i)
+        for j in succ[i]:
+            left[j] -= 1
+            est[j] = max(est[j], end[i] + (WK if nodes[j]["eng"] != e else WS))
+            if left[j] == 0:
+                ready.setdefault(nodes[j]["eng"], set()).add(j)
+    return order, extra, max(end)
+
+
+def helpers(core, nxt, topo):
+    cs = [c for c in topo.cores_of(core) if c != core and topo.may_write(c, nxt)]
+    same = [c for c in cs if topo.die(c) == topo.die(core)]
+    other = [c for c in cs if topo.die(c) != topo.die(core)]
+    return [same[0], other[0]]
+
+
+def mask8(topo, a, b):
+    m = 0
+    for e in topo.engines(a, b)[:8]:
+        m |= 1 << e
+    return m
+
+
+def hand_on(g, core, T, topo, rank, which):
+    cores = T.cores
+    me = cores[rank]
+    nr = (rank + 1) % len(cores)
+    nxt = cores[nr]
+    nh = helpers(nxt, cores[(nr + 1) % len(cores)], topo)[which]
+    lo = [0]
+
+    def send(dst, o, i, sem):
+        rid, pid = topo.addr(dst, core)
+        g.remote_dma(o, i, T.sem[sem], T.sem.lo, pid, rid, mask8(topo, core, dst))
+        lo[0] += 8
+
+    def base(t):
+        a = t * K + which * n
+        b = T.bl[:, a:a + n]
+        g.wait_ge(T.sem["hb%d" % t], len(topo.engines(me, core)) if t == 0 else 8)
+        if t < NT - 1:
+            send(nh, T.bl[:, a + K:a + K + n], b, "hb%d" % (t + 1))
+        if t > 0:
+            send(me, b, b, "b%d_%d" % (t, which))
+    p, buf = (("s", T.stl), ("z", T.zl))[which]
+    base(0)
+    for t in range(1, NT):
+        base(t)
+        for c in range(NC):
+            a = t * K + c * n
+            g.wait_ge(T.sem["h%s%d_%d" % (p, t, c)], len(topo.engines(me, core)))
+            send(nxt, buf[:, a:a + n], buf[:, a:a + n], "%s%d_%d" % (p, t, c))
+    g.wait_ge(T.sem.lo, lo[0])
+
+
+def rank_program(g, core, T, topo):
+    cores = T.cores
+    NR = len(cores)
+    rank = T.rank_of(core)
+    if rank is None:
+        for r in range(NR):
+            if core in topo.cores_of(cores[r]):
+                hs = helpers(cores[r], cores[(r + 1) % NR], topo)
+                if core in hs:
+                    hand_on(g, core, T, topo, r, hs.index(core))
+        return
+    hs = helpers(core, cores[(rank + 1) % NR], topo)
+    V, S, PE, SY = g.vector, g.scalar, g.tensor, g.sync
+    BON = [0.0]
+    nodes = []
+    lastw, readers = {}, {}
+
+    def add(eng, cost, fn, R=(), W=(), B=(), sem=None):
+        i = len(nodes)
+        deps = set()
+        for r in R:
+            if r in lastw:
+                deps.add(lastw[r])
+        for w in W:
+            if w in lastw:
+                deps.add(lastw[w])
+            deps.update(readers.get(w, ()))
+        deps.discard(i)
+        for r in R:
+            readers.setdefault(r, []).append(i)
+        for w in W:
+            lastw[w] = i
+            readers[w] = []
+        kn = eng + (W[0] if W else "-")
+        for p in ("xs", "xz", "cst"):
+            if kn[1:].startswith(p):
+                kn = eng + p + kn[2 + len(p):]
+        nodes.append(dict(eng=eng, cost=cost, fn=fn, deps=sorted(deps), banks=tuple(B), sem=sem, bonus=BON[0], grp=0, kn=kn))
+        return i
+
+    def vts(out, i0, s1, s2, o1, o2, cost, R, W, B=()):
+        if o2 is None:
+            add("V", cost, lambda: [V.tensor_scalar(out, i0, s1, None, o1)], R, W, B)
+        else:
+            add("V", cost, lambda: [V.tensor_scalar(out, i0, s1, s2, o1, o2)], R, W, B)
+
+    def vtt(out, a, b, op, cost, R, W, B=()):
+        add("V", cost, lambda: [V.tensor_tensor(out, a, b, op)], R, W, B)
+
+    def vcp(out, a, cost, R, W, B=()):
+        add("V", cost, lambda: [V.tensor_copy(out, a)], R, W, B)
+
+    def act(out, a, fn, cost, R, W, B=(), bias=0.0, scale=1.0):
+        add("S", cost + SX, lambda: [S.activation(out, a, fn, bias=bias, scale=scale)], R, W, B)
+
+    def mms(lst, R, W, B, first=True, last=True):
+        def fn():
+            r = []
+            for q, (o, l, x, _) in enumerate(lst):
+                r.append(PE.matmul(o, l, x, first and q == 0, last and q == len(lst) - 1))
+            return r
+        i = add("P", pc(*[y[3] for y in lst]), fn, R, W, B)
+        nodes[i].update(grp=(0 if last else 1) if first else (3 if last else 2))
+
+    def mset(ap, v, m, W):
+        add("V", vc(m), lambda: [V.memset(ap, v)], (), W)
+
+    def load(q, name, out, cost):
+        eng = {"S": S, "Y": SY}[q]
+        add("net", cost, None, (), (name,), sem=("ld_" + name, 16))
+        eng.dma_start(out, T[name][:, :]).then_inc(T.sem["ld_" + name], 16)
+    load("S", "xt", T.tab[:, :], 9000)
+    load("Y", "stk", T.stkI[:, :], 3000)
+    load("Y", "z", T.zl[:, 0:K], 3500)
+    load("Y", "w", T.wI[:, :], 4000)
+    load("Y", "bas", T.basI[:, :], 4500)
+    load("Y", "ln", T.lnI[:, :], 5000)
+    load("Y", "con", T.conI[:, :], 5500)
+
+    def iota(out, pat, base, cm, m, W):
+        add("G", 130 + 2 * CY * m, lambda: [g.iota(out, pat, base, cm)], (), W)
+    ib, fb = T.ib, T.fb
+    iota(T.pi[:, 0:1], [[1, 1]], 0, 1, 1, ("pi0",))
+    iota(ib[:, 128:256], [[-16, 8], [0, 16]], 0, 1, 128, ("GM",))
+    iota(ib[:, 256:384], [[0, 8], [1, 16]], 1, 0, 128, ("MI",))
+    iota(ib[:, 0:128], [[-1, 128]], 0, 1, 128, ("FQ",))
+    iota(T.ki[:, :], [[16, 16]], 0, 0, 16, ("ki",))
+    iota(T.E8i[:, :], [[1, 8], [0, 16]], 0, -1, 128, ("E8i",))
+
+    def cmx(j):
+        return T.cm[:, j * 128:(j + 1) * 128]
+    BD, Ib, nI, U, BDh, BD8, I264, ONE, nUN, I2kb, nI32, I128 = [cmx(j) for j in range(12)]
+
+    def Sr(r):
+        return T.S[:, r * 128:(r + 1) * 128]
+
+    def Wr(r):
+        return T.Wm[:, r * 128:(r + 1) * 128]
+
+    def Ro(r):
+        return T.Rot[:, r * 128:(r + 1) * 128]
+    I16 = Ro(0)
+    pf = T.pf
+    vts(T.pi[:, 1:2], T.pi[:, 0:1], 15, None, A.bitwise_and, None, vc(1), ("pi0",), ("pi1",))
+    vcp(pf[:, 0:1], T.pi[:, 1:2], vc(1), ("pi1",), ("pc",))
+    vts(pf[:, 1:2], pf[:, 0:1], 8.0, 1.0, A.mult, A.add, vc(1), ("pc",), ("p81",))
+    vts(pf[:, 2:3], pf[:, 0:1], -8.0, 124.0, A.mult, A.add, vc(1), ("pc",), ("p124",))
+    vts(pf[:, 3:4], pf[:, 0:1], VR + 0.5, 6.5, A.is_lt, A.mult, vc(1), ("pc",), ("th1",))
+    vts(pf[:, 4:5], pf[:, 0:1], 0.5, 90.0, A.is_lt, A.mult, vc(1), ("pc",), ("th2",))
+    vtt(pf[:, 5:6], pf[:, 3:4], pf[:, 4:5], A.add, vc(1), ("th1", "th2"), ("th3",))
+    vts(pf[:, 6:7], pf[:, 5:6], -1.0, -3.0, A.mult, A.add, vc(1), ("th3",), ("thr",))
+    vts(pf[:, 10:11], pf[:, 0:1], -1.0, None, A.mult, None, vc(1), ("pc",), ("pneg",))
+    vts(pf[:, 7:8], pf[:, 0:1], 14.5, -128.0, A.is_gt, A.mult, vc(1), ("pc",), ("r15a",))
+    vts(pf[:, 8:9], pf[:, 7:8], 8.0, None, A.add, None, vc(1), ("r15a",), ("r15",))
+    vcp(pf[:, 9:10], T.wI[:, :], vc(1), ("w",), ("wf",))
+    vts(fb[:, 0:128], ib[:, 128:256], 0.0, None, A.is_ge, None, vc(128), ("GM",), ("f0",))
+    vts(fb[:, 128:256], ib[:, 128:256], 15.0, None, A.is_le, None, vc(128), ("GM",), ("f1",))
+    vtt(BD, fb[:, 0:128], fb[:, 128:256], A.mult, vc(256), ("f0", "f1"), ("BD",))
+    vtt(T.kb2 if False else T.GEc0[:, 0:128], ib[:, 256:384], BD, A.mult, vc(256), ("MI", "BD"), ("E1",))
+    vts(ib[:, 384:512], ib[:, 0:128], 15, None, A.bitwise_and, None, vc(128), ("FQ",), ("FA",))
+    vts(fb[:, 256:384], ib[:, 384:512], 1.0, None, A.add, None, vc(128), ("FA",), ("f2",))
+    vtt(T.GEc0[:, 128:256], fb[:, 256:384], BD, A.mult, vc(256), ("f2", "BD"), ("F1",))
+    vts(Ib, T.GEc0[:, 128:256], 1.0, None, A.is_equal, None, vc(64), ("F1",), ("Ib",))
+    def mul(out, i, s, R, W):
+        act(out, i, F.Copy, vc(128), R, W, scale=s)
+    mul(nI, Ib, -1.0, ("Ib",), ("nI",))
+    for r in range(16):
+        vts(Sr(r), T.GEc0[:, 0:128], r + 1.0, None, A.is_equal, None, vc(64), ("E1",), ("S%d" % r,))
+    SALL = tuple("S%d" % r for r in range(16))
+    vts(fb[:, 0:128], ib[:, 0:128], 0.0, None, A.is_le, None, vc(128), ("FQ",), ("f0",))
+    vtt(U, fb[:, 0:128], BD, A.mult, vc(256), ("f0", "BD"), ("U",))
+    for r in range(16):
+        vts(Ro(r), T.GEc0[:, 128:256], r + 1.0, None, A.is_equal, None, vc(64), ("F1",), ("Ro%d" % r,))
+    for h in range(4):
+        act(T.Wm[:, h * 512:(h + 1) * 512], T.S[:, h * 512:(h + 1) * 512], F.Copy, vc(512), SALL + ("wf",), ("Wm%d" % h,), scale=pf[:, 9:10])
+    mul(nUN, Ib, -8192.0, ("Ib",), ("nUN",))
+    mul(I2kb, Ib, 2048.0, ("Ib",), ("I2kb",))
+    mul(nI32, Ib, -32.0, ("Ib",), ("nI32",))
+    mul(I128, Ib, float(n), ("Ib",), ("I128",))
+    mul(BDh, BD, pf[:, 8:9], ("BD", "r15"), ("BDh",))
+    mul(BD8, BD, 8.0, ("BD",), ("BD8",))
+    mul(I264, Ib, float(CD), ("Ib",), ("I264",))
+    mul(T.I2k[:, :], I16, 2048.0, ("Ro0",), ("I2k",))
+    mset(ONE, 1.0, 64, ("ONE",))
+    vts(T.E8[:, :], T.E8i[:, :], 0.0, None, A.is_equal, None, vc(128), ("E8i",), ("E8",))
+    kf, kb = T.kf, T.kb
+    vts(kf[:, 0:16], T.ki[:, :], pf[:, 0:1], None, A.add, None, vc(16), ("ki", "pc"), ("kf",))
+    vts(kf[:, 16:32], kf[:, 0:16], 16.0, None, A.mult, None, vc(16), ("kf",), ("k16",))
+    vcp(kb[:, 0:16], kf[:, 0:16], vc(16), ("kf",), ("kb",))
+    vcp(kb[:, 16:32], kf[:, 16:32], vc(16), ("k16",), ("kb16",))
+    vts(kf[:, 32:48], kf[:, 16:32], 15.5, None, A.add, None, vc(16), ("k16",), ("k16h",))
+    mset(kb[:, 32:48], 16.0, 16, ("kb6",))
+    mset(T.smask[:, :], 1.0, RW // 2, ("smask",))
+    mset(T.smask[:, 0:RW:16], 0.0, n, ("smask",))
+    for t in range(NT):
+        mset(T.cst[:, t * n:(t + 1) * n], 2048.0 + 4096.0 * (t + 1), n, ("cst%d" % t,))
+    mset(T.AW[:, 0:CD], 0.0, CD, ("AW0",))
+    for p in range(2):
+        mset(T["CW%d" % p][:, K:CD], 0.0, 8, ("CZ%d" % p,))
+        mset(T["YW%d" % p][:, K:CD], 0.0, 8, ("YZ%d" % p,))
+    for c in range(NC):
+        mset(T["Rc%d" % c][:, RW:RW + 16], 0.0, 16, ("Rz%d" % c,))
+        mset(T["Pc%d" % c][:, RW + 1:RW + 16], 0.0, 16, ("P%d" % c,))
+        mset(T["Pc%d" % c][:, 0:1], 0.0, 16, ("P%d" % c,))
+    mset(T.ac[:, 0:1], 32.0 * 248, 1, ("A32",))
+    for c in range(NC):
+        vcp(T.stl[:, c * n:(c + 1) * n], T.stkI[:, c * n:(c + 1) * n], vc(n), ("stk",), ("st0_%d" % c,))
+    for c in range(NC):
+        vts(T.bl[:, c * n:(c + 1) * n], T.basI[:, c * n:(c + 1) * n], -2048.0, None, A.add, None, vc(n), ("bas",), ("b0_%d" % c,))
+    lo = [0]
+
+    def send(dst, o, i, sem, R, W):
+        rid, pid = topo.addr(dst, core)
+        m = topo.mask(core, dst)
+        lo[0] += len(topo.engines(core, dst))
+
+        def fn():
+            g.remote_dma(o, i, T.sem[sem], T.sem.lo, pid, rid, m)
+            return []
+        add("G", 1500, fn, R, W)
+    for c in range(NC):
+        send(hs[c], T.bl[:, c * n:(c + 1) * n], T.bl[:, c * n:(c + 1) * n], "hb0", ("b0_%d" % c,), ("snt%d" % c,))
+    pz = T.pz
+    vcp(T.lnB[:, :], T.lnI[:, :], vc(K), ("ln",), ("lnB",))
+    mms([(T.pd2[:, 0:K], T.E8[:, :], T.lnB[:, :], K)], ("E8", "lnB"), ("pd2",), ("pd2",))
+    act(T.YW0[:, 0:K], T.pd2[:, 0:K], F.Identity, vc(K), ("pd2",), ("Y0",), ("pd2",), bias=-6.0, scale=8.0)
+    vts(T.lm0[:, :], T.pd2[:, 0:K], pf[:, 0:1], None, A.is_gt, None, vc(K), ("pd2", "pc"), ("lm0",), ("pd2",))
+    vtt(T.CW0[:, 0:K], T.conI[:, :], T.lm0[:, :], A.mult, vc(2 * K), ("con", "lm0"), ("C0",))
+    vcp(pz[:, 256:512], T.conI[:, :], vc(K), ("con",), ("full",), ("pz",))
+    for t in range(1, NT):
+        for c in range(NC):
+            add("net", LAT * t, None, ("snt%d" % c,), ("b%d_%d" % (t, c),), sem=("b%d_%d" % (t, c), 8))
+
+    rotp = [0]
+
+    def chunk(t, c):
+        q = "_%d" % c
+        st, z = "st%d_%d" % (t, c), "z%d_%d" % (t, c)
+        if t == 0:
+            z = "z"
+        a0 = t * K + c * n
+        stA, zA, bA = T.stl[:, a0:a0 + n], T.zl[:, a0:a0 + n], T.bl[:, a0:a0 + n]
+        X = {k: T[k + "c%d" % c] for k in ("R", "P", "GE", "hit", "nf", "AM", "xh", "sb", "rotW", "rg", "pm", "yg", "nmp", "rotK", "baM", "wi", "wf", "wl", "pvb")}
+        pa, pw = T["pa%d" % c], T["pw%d" % c]
+        PA, PW = ("pa%d" % c,), ("pw%d" % c,)
+        par = t % 2
+        CW, YW = T["CW%d" % par], T["YW%d" % par]
+        k0 = c * n
+
+        def k(*xs):
+            return tuple(x + q for x in xs)
+
+        def wi(j):
+            return X["wi"][:, j * W1:(j + 1) * W1]
+
+        def wf(j):
+            return X["wf"][:, j * W1:(j + 1) * W1]
+
+        def wl(j):
+            return X["wl"][:, j * W1:(j + 1) * W1]
+
+        def pwx(j):
+            return pw[:, j * W1:(j + 1) * W1]
+        zP = pz[:, k0:k0 + n]
+        mms([(zP, Ib, zA, n)], ("Ib", z), k("zP"), ("pz",))
+        tab = T.tab[:, 0:4096]
+        R = X["R"]
+        RR = ()
+        for qi, (ge, x0, x1) in enumerate(GSPLIT):
+            o, w = R[:, 16 * x0:16 * x1], tab.indirect(T.stl[:, a0 + x0:a0 + x1])
+            if ge == "V":
+                add("V", gc_(16 * (x1 - x0)), lambda o=o, w=w: [V.tensor_copy(o, w)], ("xt", st), k("R%d" % qi))
+            else:
+                act(o, w, F.Identity, gc_(16 * (x1 - x0)), ("xt", st), k("R%d" % qi))
+            RR += k("R%d" % qi)
+        vts(X["sb"][:, :], stA, -2048.0, None, A.add, None, vc(n / 2), (st,), k("sb"))
+        GE = X["GE"]
+        if t == 0 and c == 0:
+            RR0 = RR + tuple("Ro%d" % r for r in range(16)) + SALL
+        GEs = []
+        i0 = VR + 1
+        grp = 0
+        vrow = list(range(1, VR + 1))
+        first = [True]
+        srows = []
+        while i0 < 16:
+            srows.append(list(range(i0, min(16, i0 + 4))))
+            i0 += 4
+        for rows in srows:
+            x = rotp[0] % 3
+            rotp[0] += 1
+            pd = T["pd%d" % x]
+
+            def fn(rows=rows, pd=pd):
+                r = []
+                for jj, i in enumerate(rows):
+                    o = pd[:, jj * n:(jj + 1) * n]
+                    r.append(PE.matmul(o, Ib, R[:, i:RW:16], True, False))
+                    r.append(PE.matmul(o, nI, zA, False, True))
+                return r
+            add("P", pc(*([n] * 2 * len(rows))), fn, RR + ("Ib", "nI", z), ("pd%d" % x,), ("pd%d" % x,))
+            act(GE[:, rows[0] * n:(rows[-1] + 1) * n], pd[:, 0:len(rows) * n], F.Sign, vc(len(rows) * n), ("pd%d" % x,), k("GE%d" % rows[0]) + (("E1", "F1") if t == 0 and c == 0 else ()), ("pd%d" % x,), bias=0.5)
+        for i in vrow:
+            vtt(GE[:, i * n:(i + 1) * n], R[:, i:RW:16], zP, A.is_ge, vc(n), RR + k("zP"), k("GE%d" % i) + (("E1", "F1") if t == 0 and c == 0 else ()), ("pz",))
+        parts = [vrow] + srows
+        vo = pa[:, 0:n]
+        for j, rows in enumerate(parts):
+            keys = k(*["GE%d" % i for i in rows]) if j == 0 else k("GE%d" % rows[0])
+            mms([(vo, Sr(i), GE[:, i * n:(i + 1) * n], n) for i in rows], keys + SALL, k("votes"), PA, j == 0, j == len(parts) - 1)
+        if HV[c]:
+            vts(X["hit"][:, :], vo, pf[:, 6:7], 0.0, A.add, A.is_ge, vc(n), k("votes") + ("thr",), k("hit"), PA)
+        else:
+            act(X["hit"][:, :], vo, F.Sign, vc(n), k("votes") + ("thr",), k("hit"), PA, bias=pf[:, 6:7])
+        co = pa[:, n:2 * n]
+        mms([(co, U, X["hit"][:, :], n)], k("hit") + ("U",), k("C"), PA)
+        if HV[c]:
+            vts(X["nf"][:, :], co, 0.5, None, A.is_lt, None, vc(n), k("C"), k("nf"), PA)
+        else:
+            act(X["nf"][:, :], co, F.Relu, vc(n), k("C") + ("pneg",), k("nf"), PA, bias=pf[:, 10:11], scale=-1.0)
+        for h in range(2):
+            s0, s1 = h * RW // 2, (h + 1) * RW // 2
+            add("V", vc(RW / 4), lambda s0=s0, s1=s1: [V.tensor_tensor_scan(X["P"][:, 1 + s0:1 + s1], T.smask[:, s0:s1], R[:, s0:s1], 0.0, A.mult, A.max)], RR + ("smask",), ("P%d%s" % (c, "ab"[h]),))
+        for b4 in range(16 // RWN):
+            x = rotp[0] % 3
+            rotp[0] += 1
+            pd = T["pd%d" % x]
+
+            def fn(pd=pd, b4=b4):
+                return [PE.matmul(pd[:, jj * n:(jj + 1) * n], Ro(RWN * b4 + jj), X["sb"][:, :], True, True) for jj in range(RWN)]
+            add("P", pc(*([n] * RWN)), fn, k("sb") + tuple("Ro%d" % r for r in range(16)), ("pd%d" % x,), ("pd%d" % x,))
+            act(X["rotW"][:, b4 * RWN * n:(b4 + 1) * RWN * n], pd[:, 0:RWN * n], F.Copy, vc(RWN * n), ("pd%d" % x,), k("rw%d" % b4), ("pd%d" % x,))
+        nf = X["nf"]
+        mms([(pwx(0), Ib, kb[:, 16:16 + W1], W1)] + [(pwx(0), Sr(r), nf[:, r:n:16], W1) for r in range(16)], k("nf") + ("Ib", "kb16") + SALL, k("hw"), PW)
+        vcp(wl(0), pwx(0), vc(8), k("hw"), k("l1"), PW)
+        vtt(T.unb[:, c * 8:c * 8 + 8], pwx(0), kf[:, 32:32 + W1], A.is_ge, vc(8), k("hw") + ("k16h",), k("unb"), PW)
+        vts(wf(2), pwx(0), 128.0, None, A.mult, None, vc(8), k("hw"), k("h128"), PW)
+        AM = X["AM"]
+        add("V", gc_(n), lambda: [V.tensor_copy(AM[:, n:2 * n], X["P"][:, :].indirect(wl(0)))], k("l1") + ("P%da" % c, "P%db" % c, "P%d" % c), k("M"))
+        act(X["xh"][:, :], R[:, :].indirect(wl(0)), F.Identity, gc_(n), k("l1") + RR + ("Rz%d" % c,), k("xh"))
+        mms([(pwx(1), Ib, kb[:, 32:32 + W1], W1)] + [(pwx(1), Wr(r), AM[:, n + r:2 * n:16], W1) for r in range(16)], k("M") + ("Wm0", "Wm1", "Wm2", "Wm3", "Ib", "kb6"), k("uw"), PW)
+        mms([(pwx(2), Sr(r), X["xh"][:, r:n:16], W1) for r in range(16)] + [(pwx(2), nUN, T.unb[:, c * 8:c * 8 + 8], W1)], k("xh", "unb") + SALL + ("nUN",), k("vw"), PW)
+        uv = X["wi"][:, 4 * W1:6 * W1]
+        vts(uv, pw[:, W1:3 * W1], 0.0, None, A.max, None, vc(16), k("uw", "vw"), k("ui"), PW)
+        vts(wi(1), wi(4), 4095, None, A.bitwise_and, None, vc(8), k("ui"), k("uc"))
+        vtt(wi(2), wi(1), wi(1), A.mult, vc(8), k("uc"), k("uq"))
+        vts(wi(3), wi(2), T.ac[:, 0:1], None, A.add, None, vc(8), k("uq") + ("A32",), k("ur"))
+        vts(wi(0), wi(3), 5, 255, A.arith_shift_right, A.bitwise_and, vc(8), k("ur"), k("uj"))
+        vts(wi(6), wi(5), 3, None, A.bitwise_and, None, vc(8), k("ui"), k("v3"))
+        vts(X["pvb"][:, :], wi(6), 1.0, None, A.min, None, vc(8), k("v3"), k("pvb"))
+        vts(wf(3), X["pvb"][:, :], -256.0, 256.0, A.mult, A.add, vc(8), k("pvb"), k("np"))
+        vtt(wi(7), wi(0), wf(3), A.max, vc(8), k("uj", "np"), k("um"))
+        vcp(wl(1), wi(7), vc(8), k("um"), k("lj"))
+        act(X["yg"][:, :], YW[:, 0:CD].indirect(wl(1)), F.Identity, gc_(n), k("lj") + ("Y%d" % par, "YZ%d" % par), k("yg"))
+        act(X["pm"][:, :], CW[:, 0:CD].indirect(wl(1)), F.Identity, gc_(n), k("lj") + ("C%d" % par, "CZ%d" % par), k("pm"), bias=-2048.0)
+        mms([(pwx(3), I2kb, kb[:, 0:W1], W1), (pwx(3), nI, kb[:, 0:W1], W1), (pwx(3), nI32, X["pvb"][:, :], W1)] + [(pwx(3), Sr(r), X["yg"][:, r:n:16], W1) for r in range(16)],
+            k("yg", "pvb") + SALL + ("I2kb", "nI", "nI32", "kb"), k("mw"), PW)
+        vtt(wi(8), wf(2), pwx(3), A.subtract, vc(8), k("h128", "mw"), k("x1"), PW)
+        vts(wi(9), wi(8), RW - 1, None, A.bitwise_and, None, vc(8), k("x1"), k("x2"))
+        vcp(wl(2), wi(9), vc(8), k("x2"), k("lr"))
+        act(X["rg"][:, :], X["rotW"][:, :].indirect(wl(2)), F.Identity, gc_(n), k("lr", *["rw%d" % b for b in range(16 // RWN)]), k("rg"))
+        hy = pa[:, 2 * n:3 * n]
+        mms([(hy, BDh, nf[:, :], n), (hy, nI, X["yg"][:, :], n)], k("nf", "yg") + ("BDh", "nI"), k("hy"), PA)
+        vts(X["nmp"][:, :], X["yg"][:, :], pf[:, 1:2], None, A.is_lt, None, vc(n / 2), k("yg") + ("p81",), k("nmp"))
+        vts(hy, hy, pf[:, 2:3], None, A.is_ge, None, vc(n), k("hy") + ("p124",), k("hy"), PA)
+        vtt(vo, X["nmp"][:, :], hy, A.subtract, vc(n), k("nmp", "hy"), k("votes"), PA)
+        vtt(X["baM"][:, :], bA, hy, A.mult, vc(n), k("hy") + ("b%d_%d" % (t, c),), k("baM"), PA)
+        no = pa[:, 3 * n:4 * n]
+        mms([(no, I16, X["pm"][:, :], n), (no, T.I2k[:, :], X["nmp"][:, :], n), (no, I16, X["baM"][:, :], n)], k("pm", "nmp", "baM") + ("Ro0", "I2k"), k("new"), PA, True, False)
+        vtt(X["rotK"][:, :], X["rg"][:, :], vo, A.mult, vc(n), k("rg", "votes"), k("rotK"), PA)
+        mms([(no, I16, X["rotK"][:, :], n)], k("rotK") + ("Ro0",), k("new"), PA, False, True)
+        if t < NT - 1:
+            so = T.sto[:, a0:a0 + n]
+            vts(so, no, 2048.0, None, A.add, None, vc(n), k("new"), k("so"), PA)
+            send(hs[0], T.stl[:, a0 + K:a0 + K + n], so, "hs%d_%d" % (t + 1, c), k("so"), ("xs%d_%d" % (t, c),))
+            add("net", LAT, None, ("xs%d_%d" % (t, c),), ("st%d_%d" % (t + 1, c),), sem=("s%d_%d" % (t + 1, c), 8))
+        else:
+            vts(T.stf[:, k0:k0 + n], no, 2048.0, None, A.add, None, vc(n), k("new"), k("so"), PA)
+        mms([(pwx(4), Ib, kb[:, 0:W1], W1), (pwx(4), I128, T.unb[:, c * 8:c * 8 + 8], W1)], k("unb") + ("Ib", "kb", "I128"), k("mk"), PW)
+        vcp(wl(3), pwx(4), vc(8), k("mk"), k("lm"), PW)
+        mms([(co, Ib, X["xh"][:, :], n), (co, nI, zA, n)], k("xh") + ("Ib", "nI", z), k("C"), PA)
+        act(AM[:, 0:n], co, F.Abs, vc(n), k("C"), k("ad"), PA)
+        zo = T.zo[:, a0:a0 + n]
+        act(zo, AM[:, :].indirect(wl(3)), F.Identity, gc_(n), k("lm", "ad", "M"), k("zo"))
+        if t < NT - 1:
+            send(hs[1], T.zl[:, a0 + K:a0 + K + n], zo, "hz%d_%d" % (t + 1, c), k("zo"), ("xz%d_%d" % (t, c),))
+            add("net", LAT, None, ("xz%d_%d" % (t, c),), ("z%d_%d" % (t + 1, c),), sem=("z%d_%d" % (t + 1, c), 8))
+
+    def tail(t):
+        par = t % 2
+        CW, YW, CN, YN = T["CW%d" % par], T["YW%d" % par], T["CW%d" % (1 - par)], T["YW%d" % (1 - par)]
+        for c in range(NC):
+            q = "_%d" % c
+            X = {k: T[k + "c%d" % c] for k in ("nf", "AM", "sb", "wi", "wl", "pvb", "told", "tnew")}
+            pa, pw = T["pa%d" % c], T["pw%d" % c]
+            PW = ("pw%d" % c,)
+            k0 = c * n
+
+            def k(*xs):
+                return tuple(x + q for x in xs)
+            if t < NT - 1:
+                wi1 = X["wi"][:, 4 * W1:5 * W1]
+                w11, w12 = X["wi"][:, 11 * W1:12 * W1], X["wi"][:, 12 * W1:13 * W1]
+                la = X["wl"][:, 4 * W1:5 * W1]
+                vts(w11, wi1, 15, None, A.bitwise_and, None, vc(8), k("ui"), k("t1"))
+                vtt(w12, w11, kf[:, 16 + c * W1:16 + (c + 1) * W1], A.add, vc(8), k("t1") + ("k16",), k("t2"))
+                vcp(la, w12, vc(8), k("t2"), k("la"))
+                add("V", gc_(n), lambda X=X, la=la: [V.tensor_tensor(X["told"][:, :], T.tab[:, 0:4096].indirect(la), X["AM"][:, n:2 * n], A.add)], k("la", "M") + ("xt",), k("told"))
+                vts(X["tnew"][:, :], X["told"][:, :], 1, None, A.arith_shift_right, None, vc(n), k("told"), k("tnew"))
+                add("V", 60 + 3.8 * CY * n, lambda X=X, la=la: [V.tensor_copy(T.tab[:, 0:4096].indirect(la), X["tnew"][:, :])], k("la", "tnew"), ("xt",))
+            sl = T.pw0[:, 80 + c * W1:80 + (c + 1) * W1]
+            mms([(sl, Ib, kb[:, c * W1:(c + 1) * W1], W1), (sl, I264, X["pvb"][:, :], W1)], k("pvb") + ("Ib", "I264", "kb"), k("sl"), ("pw0",))
+            SS, hB = pw[:, 128:256], pw[:, 256:384]
+            mms([(SS, I16, X["sb"][:, :], n), (SS, I16, T.cst[:, t * n:(t + 1) * n], n)], k("sb") + ("Ro0", "cst%d" % t), k("SS"), PW)
+            mms([(hB, BD8, X["nf"][:, :], n)], k("nf") + ("BD8",), k("hB"), PW)
+            aw = T.AW[:, CD + k0:CD + k0 + n]
+            vtt(aw, X["nf"][:, :], SS, A.mult, vc(n), k("nf", "SS"), k("aw"), PW)
+            if t < NT - 1:
+                act(CW[:, CD + k0:CD + k0 + n], aw, F.Relu, vc(n), k("aw"), k("cc"), (), bias=-4096.0 * (t + 1))
+            act(YW[:, CD + k0:CD + k0 + n], hB, F.Identity, vc(n), k("hB"), k("yc"), PW, bias=-6.0)
+        sel = T.sel[:, :]
+        SEL = ("sel",)
+        vcp(sel, T.pw0[:, 80:80 + K // 16], vc(16), ("sl_0", "sl_1"), SEL, ("pw0",))
+        act(YN[:, 0:K], YW[:, :].indirect(sel), F.Identity, gc_(K), SEL + ("Y%d" % par, "YZ%d" % par, "yc_0", "yc_1"), ("Y%d" % (1 - par),))
+        if t < NT - 1:
+            act(CN[:, 0:K], CW[:, :].indirect(sel), F.Identity, gc_(K), SEL + ("C%d" % par, "CZ%d" % par, "cc_0", "cc_1"), ("C%d" % (1 - par),))
+        act(T.asel[:, :], T.AW[:, :].indirect(sel), F.Identity, gc_(K), SEL + ("AW0", "aw_0", "aw_1"), ("asel",))
+        vtt(pz[:, 256:512], T.asel[:, :], pz[:, 256:512], A.max, vc(K), ("asel", "full"), ("full",), ("pz",))
+        if t < NT - 1:
+            to = T.pw0[:, 64:80]
+            mms([(to, ONE, T.unb[:, :], 16)], ("unb_0", "unb_1", "ONE"), ("tot",), ("pw0",))
+            add("V", vc(16), lambda: [V.tensor_reduce(T.ac[:, 1:2], to, AxisListType.X, A.add)], ("tot",), ("ac1",), ("pw0",))
+            vts(T.ai[:, 0:1], T.ac[:, 1:2], 248.0, None, A.add, None, vc(1), ("ac1",), ("ai0",))
+            vts(T.ai[:, 1:2], T.ai[:, 0:1], 255, None, A.bitwise_and, None, vc(1), ("ai0",), ("ai1",))
+            vts(T.ac[:, 0:1], T.ai[:, 1:2], 32.0, None, A.mult, None, vc(1), ("ai1",), ("A32",))
+
+    for t in range(NT):
+        for c in range(NC):
+            BON[0] = BONUS * (1 - c)
+            chunk(t, c)
+        BON[0] = 0.0
+        tail(t)
+    outs = [0]
+
+    def store(out, i, R):
+        def fn():
+            SY.dma_start(out, i).then_inc(T.sem.outs, 16)
+            return []
+        outs[0] += 16
+        add("Y", 100, fn, R, ())
+    store(T.yz[:, :], T.zo[:, (NT - 1) * K:NT * K], ("zo_0", "zo_1"))
+    store(T.ys[:, :], T.stf[:, :], ("so_0", "so_1"))
+    yo = T.pa0[0:8, 0:K]
+    mms([(yo, T.S[:, 0:128:16], T["YW%d" % (NT % 2)][:, 0:K], K)], SALL + ("Y%d" % (NT % 2), "votes_0", "C_0"), ("yo", "votes_0", "C_0"), ("pa0",))
+    vts(T.ynf[:, :], yo, 96.0, 1.0 / 128, A.add, A.mult, vc(K), ("yo",), ("ynf",), ("pa0",))
+    store(T.yn[:, :], T.ynf[:, :], ("ynf",))
+    vcp(T.yci[:, :], pz[:, 256:512], vc(K), ("full",), ("yci",), ("pz",))
+    vts(T.ycj[:, :], T.yci[:, :], 4095, None, A.bitwise_and, None, vc(K), ("yci",), ("ycj",))
+    vcp(T.ycf[:, :], T.ycj[:, :], vc(K), ("ycj",), ("ycf",))
+    store(T.yc[:, :], T.ycf[:, :], ("ycf",))
+
+    if "o" not in ORDERS:
+        seen_kn = {}
+        for x in nodes:
+            seen_kn[x["kn"]] = seen_kn.get(x["kn"], 0) + 1
+        names = sorted(q for q, m in seen_kn.items() if m >= 4 and q[0] in "VSPG")
+        for x in nodes:
+            if BTS and x["kn"] in names:
+                x["bonus"] += 800.0 * (LEV.index(BTS[names.index(x["kn"])]) - 32)
+        ORDERS["o"] = schedule(nodes)
+    order, extra, _ = ORDERS["o"]
+    Q = {"V": V, "S": S, "P": PE, "G": g, "Y": SY}
+    SM = {"V": "sV", "S": "sS", "P": "sP", "G": "sG"}
+    cnt = {"V": 0, "S": 0, "P": 0, "G": 0}
+    done = {}
+    seen = {e: {} for e in Q}
+    for i in order:
+        x = nodes[i]
+        if x["sem"]:
+            done[i] = [x["sem"]]
+            continue
+        if x["fn"] is None:
+            done[i] = []
+            continue
+        e = x["eng"]
+        need = {}
+        for d in tuple(x["deps"]) + extra[i]:
+            for s, v in done[d]:
+                need[s] = max(need.get(s, 0), v)
+        for s, v in sorted(need.items()):
+            if seen[e].get(s, 0) < v:
+                Q[e].wait_ge(T.sem[s], v)
+                seen[e][s] = v
+        r = x["fn"]()
+        for ins in r:
+            cnt[e] += 1
+            ins.then_inc(T.sem[SM[e]], 1)
+        done[i] = [(SM[e], cnt[e])] if r else []
+    SY.wait_ge(T.sem.outs, outs[0])
+    for e in cnt:
+        g.wait_ge(T.sem[SM[e]], cnt[e])
+    g.wait_ge(T.sem.lo, lo[0])

@@ -1,59 +1,49 @@
-from concourse.bass import DstId, RemoteDMATransfer
-from concourse.mybir import dt, AluOpType as A, AxisListType, ActivationFunctionType as F
+from concourse.mybir import AluOpType as A, AxisListType, ActivationFunctionType as F
 
 NT = 5
 K = 256
 NC = 2
 n = K // NC
-VR = 7
-GSPLIT = (("V", 0, 64), ("S", 64, 128))
-LAT = 5000
-HV = (1, 1)
-LEV = "ABCDEFGHIJKLMNOPQRSTUVWXYZabcdefghijklmnopqrstuvwxyz0123456789+-"
-BTS = "Oo0QdjyyhW1pc1f-lxmQhgihFAjggew-SI0d1spaomGwWOZond35Axiz38ozCijsFKvg-jznb+qk-lqv7gbdZNpd6cGrhqyav7nf5e-3nNTzpsUdspvcbdcpdowVRQP3OeVlZ3jV-06hcaf3mcrffcwveehl8eW"
-PEC = 0.5
-SX = 80
-WS = 45
-RWN = 4
-WK = 100
-BONUS = 6000.0
-SLK = 60
-CD = 264
+H = n // 2
 W1 = n // 16
 RW = 16 * n
+CFG = dict(
+    VR=7,
+    SUB=64,
+    GATHER=(("V", 0, 32), ("S", 32, 64), ("S", 64, 128)),
+    HIT="S", NF="S", M="V", Y="S", VM="V", TOLD="S", H64="V",
+    LAT=4000, PEC=0.5, SX=80, WS=45, WK=100, BONUS=3000.0, SLK=60, XT=6000,
+)
 
 SCRATCH = {
     "tab": ("sbuf", [128, 4096], "bfloat16"),
     "stl": ("sbuf", [128, NT * K], "uint16"), "sto": ("sbuf", [128, NT * K], "uint16"),
     "zl": ("sbuf", [128, NT * K], "bfloat16"), "zo": ("sbuf", [128, NT * K], "bfloat16"),
-    "bl": ("sbuf", [128, NT * K], "float16"),
-    "stkI": ("sbuf", [128, K], "int32"), "basI": ("sbuf", [128, K], "int32"), "conI": ("sbuf", [128, K], "int32"),
+    "bl": ("sbuf", [128, NT * K], "int32"),
+    "stkI": ("sbuf", [128, K], "int32"), "conI": ("sbuf", [128, K], "int32"),
     "lnI": ("sbuf", [8, K], "int32"), "lnB": ("sbuf", [8, K], "bfloat16"), "wI": ("sbuf", [128, 1], "int32"),
     "stf": ("sbuf", [128, K], "float32"),
-    "S": ("sbuf", [128, 16 * 128], "bfloat16"), "Wm": ("sbuf", [128, 16 * 128], "float16"),
-    "Rot": ("sbuf", [128, 16 * 128], "float16"),
-    "cm": ("sbuf", [128, 12 * 128], "bfloat16"),
-    "I2k": ("sbuf", [128, 128], "float16"),
-    "E8": ("sbuf", [8, 128], "bfloat16"), "E8i": ("sbuf", [8, 128], "int32"),
-    "ib": ("sbuf", [128, 4 * 128], "int32"), "fb": ("sbuf", [128, 3 * 128], "float32"),
-    "ki": ("sbuf", [128, 16], "int32"), "kf": ("sbuf", [128, 64], "float32"), "kb": ("sbuf", [128, 64], "bfloat16"),
-    "pi": ("sbuf", [128, 2], "int32"), "pf": ("sbuf", [128, 16], "float32"),
-    "smask": ("sbuf", [128, RW], "bfloat16"), "cst": ("sbuf", [128, NT * n], "float16"),
-    "AW": ("sbuf", [128, CD + K], "float32"), "asel": ("sbuf", [128, K], "float32"),
-    "CW0": ("sbuf", [128, CD + K], "float32"), "CW1": ("sbuf", [128, CD + K], "float32"),
-    "YW0": ("sbuf", [128, CD + K], "bfloat16"), "YW1": ("sbuf", [128, CD + K], "bfloat16"),
-    "lm0": ("sbuf", [128, K], "float32"), "sel": ("sbuf", [128, 16], "uint16"), "unb": ("sbuf", [128, 16], "bfloat16"),
-    "ac": ("sbuf", [128, 8], "float32"), "ai": ("sbuf", [128, 8], "int32"),
-    "yci": ("sbuf", [128, K], "int32"), "ycj": ("sbuf", [128, K], "int32"), "ycf": ("sbuf", [128, K], "float32"), "ynf": ("sbuf", [8, K], "float32"),
+    "X": ("sbuf", [128, 144], "bfloat16"), "Xg": ("sbuf", [128, 128], "bfloat16"), "Xr": ("sbuf", [128, 128], "bfloat16"),
+    "Tb": ("sbuf", [128, 3 * 144], "bfloat16"), "Tw": ("sbuf", [128, 144], "float16"),
+    "Rot": ("sbuf", [128, 2 * 16 * 128], "float16"),
+    "cm": ("sbuf", [128, 20 * 128], "bfloat16"),
+    "E8": ("sbuf", [8, 128], "bfloat16"),
+    "pi": ("sbuf", [128, 64], "int32"), "pf": ("sbuf", [128, 48], "float32"),
+    "kf": ("sbuf", [128, 16], "float32"), "kb": ("sbuf", [128, 16], "bfloat16"),
+    "smask": ("sbuf", [128, 1024], "bfloat16"),
+    "CW0": ("sbuf", [128, 2 * K], "float32"), "CW1": ("sbuf", [128, 2 * K], "float32"),
+    "unb": ("sbuf", [128, 16], "bfloat16"), "ac": ("sbuf", [128, 8], "float32"),
+    "yci": ("sbuf", [128, K], "int32"), "ycj": ("sbuf", [128, K], "int32"), "ycf": ("sbuf", [128, K], "float32"),
+    "ycv": ("sbuf", [128, K], "bfloat16"), "ynf": ("sbuf", [8, K], "float32"),
     "pz": ("psum", [128, 512], "float32"),
 }
 for _c in range(NC):
     for _nm, _w, _d in (("R", RW + 16, "bfloat16"), ("P", RW + 16, "bfloat16"), ("GE", RW, "bfloat16"),
-                        ("hit", n, "bfloat16"), ("nf", n, "bfloat16"), ("AM", 2 * n, "bfloat16"), ("xh", n, "bfloat16"),
-                        ("sb", n, "float16"), ("rotW", RW, "float32"), ("rg", n, "float32"), ("pm", n, "float16"),
-                        ("yg", n, "bfloat16"), ("nmp", n, "float16"), ("rotK", n, "float16"),
-                        ("baM", n, "float16"), ("wi", 16 * W1, "int32"), ("wf", 16 * W1, "float32"),
-                        ("wl", 8 * W1, "uint16"), ("pvb", W1, "bfloat16"), ("told", n, "int32"), ("tnew", n, "int32")):
+                        ("hit", n, "bfloat16"), ("nf", n, "bfloat16"), ("M", n, "bfloat16"), ("y", n, "bfloat16"),
+                        ("sb", n, "float16"), ("rotW", 16 * H, "float32"), ("rg", n, "int32"), ("ru", n, "int32"),
+                        ("vm", n, "bfloat16"), ("bm", n, "float32"), ("low", n, "float32"), ("ef", n, "float32"),
+                        ("wi", 16 * W1, "int32"), ("wf", 4 * W1, "float32"), ("wl", 4 * W1, "uint16"),
+                        ("told", n, "int32"), ("thf", n, "float32"), ("tnew", n, "int32"), ("cd", n, "float32")):
         SCRATCH[_nm + "c%d" % _c] = ("sbuf", [128, _w], _d)
     SCRATCH["pa%d" % _c] = ("psum", [128, 512], "float32")
     SCRATCH["pw%d" % _c] = ("psum", [128, 512], "float32")
@@ -66,19 +56,13 @@ SEMAPHORES = (["sV", "sS", "sP", "sG", "lo", "outs"] + ["ld_" + x for x in LOADS
               + ["h%s%d_%d" % (p, t, c) for p in ("s", "z") for t in range(1, NT) for c in range(NC)]
               + ["hb%d" % t for t in range(NT)])
 
-CY = 0.83 * 1.2
-
 
 def vc(m, f=1.0):
-    return CY * max(64, m * f) + 15
+    return max(64, m * f) + 15
 
 
 def gc_(m):
-    return 60 + 1.5 * CY * m
-
-
-def pc(*ms):
-    return sum(PEC * max(64, m) for m in ms)
+    return 55 + 1.56 * m
 
 
 ORDERS = {}
@@ -109,8 +93,6 @@ def schedule(nodes):
     while len(order) < N:
         best = None
         for e, rs in ready.items():
-            if not rs:
-                continue
             f = free.get(e, 0.0)
             c = []
             for i in rs:
@@ -120,12 +102,12 @@ def schedule(nodes):
                 for b in nodes[i]["banks"]:
                     lb = bank.get(b)
                     if lb and nodes[lb]["eng"] != e:
-                        s = max(s, end[lb] + 60)
+                        s = max(s, end[lb] + CFG["WK"])
                 c.append((s, i))
             if not c:
                 continue
             m = min(c)[0]
-            k = max((pri[i], -s, i) for s, i in c if s <= m + SLK)
+            k = max((pri[i], -s, i) for s, i in c if s <= m + CFG["SLK"])
             if best is None or m < best[0]:
                 best = (m, k[2], -k[1])
         i, s = best[1], best[2]
@@ -148,7 +130,7 @@ def schedule(nodes):
         order.append(i)
         for j in succ[i]:
             left[j] -= 1
-            est[j] = max(est[j], end[i] + (WK if nodes[j]["eng"] != e else WS))
+            est[j] = max(est[j], end[i] + (CFG["WK"] if nodes[j]["eng"] != e else CFG["WS"]))
             if left[j] == 0:
                 ready.setdefault(nodes[j]["eng"], set()).add(j)
     return order, extra, max(end)
@@ -161,13 +143,6 @@ def helpers(core, nxt, topo):
     return [same[0], other[0]]
 
 
-def mask8(topo, a, b):
-    m = 0
-    for e in topo.engines(a, b)[:8]:
-        m |= 1 << e
-    return m
-
-
 def hand_on(g, core, T, topo, rank, which):
     cores = T.cores
     me = cores[rank]
@@ -178,13 +153,14 @@ def hand_on(g, core, T, topo, rank, which):
 
     def send(dst, o, i, sem):
         rid, pid = topo.addr(dst, core)
-        g.remote_dma(o, i, T.sem[sem], T.sem.lo, pid, rid, mask8(topo, core, dst))
-        lo[0] += 8
+        m = topo.mask(core, nxt)
+        g.remote_dma(o, i, T.sem[sem], T.sem.lo, pid, rid, m)
+        lo[0] += len(topo.engines(core, nxt))
 
     def base(t):
         a = t * K + which * n
         b = T.bl[:, a:a + n]
-        g.wait_ge(T.sem["hb%d" % t], len(topo.engines(me, core)) if t == 0 else 8)
+        g.wait_ge(T.sem["hb%d" % t], len(topo.engines(me, core) if t == 0 else topo.engines(core, nxt)))
         if t < NT - 1:
             send(nh, T.bl[:, a + K:a + K + n], b, "hb%d" % (t + 1))
         if t > 0:
@@ -212,7 +188,9 @@ def rank_program(g, core, T, topo):
                     hand_on(g, core, T, topo, r, hs.index(core))
         return
     hs = helpers(core, cores[(rank + 1) % NR], topo)
+    far = len(topo.engines(hs[0], cores[(rank + 1) % NR]))
     V, S, PE, SY = g.vector, g.scalar, g.tensor, g.sync
+    VR, SUB, LAT = CFG["VR"], CFG["SUB"], CFG["LAT"]
     BON = [0.0]
     nodes = []
     lastw, readers = {}, {}
@@ -221,8 +199,7 @@ def rank_program(g, core, T, topo):
         i = len(nodes)
         deps = set()
         for r in R:
-            if r in lastw:
-                deps.add(lastw[r])
+            deps.add(lastw[r])
         for w in W:
             if w in lastw:
                 deps.add(lastw[w])
@@ -233,11 +210,7 @@ def rank_program(g, core, T, topo):
         for w in W:
             lastw[w] = i
             readers[w] = []
-        kn = eng + (W[0] if W else "-")
-        for p in ("xs", "xz", "cst"):
-            if kn[1:].startswith(p):
-                kn = eng + p + kn[2 + len(p):]
-        nodes.append(dict(eng=eng, cost=cost, fn=fn, deps=sorted(deps), banks=tuple(B), sem=sem, bonus=BON[0], grp=0, kn=kn))
+        nodes.append(dict(eng=eng, cost=cost, fn=fn, deps=sorted(deps), banks=tuple(B), sem=sem, bonus=BON[0], grp=0))
         return i
 
     def vts(out, i0, s1, s2, o1, o2, cost, R, W, B=()):
@@ -253,122 +226,148 @@ def rank_program(g, core, T, topo):
         add("V", cost, lambda: [V.tensor_copy(out, a)], R, W, B)
 
     def act(out, a, fn, cost, R, W, B=(), bias=0.0, scale=1.0):
-        add("S", cost + SX, lambda: [S.activation(out, a, fn, bias=bias, scale=scale)], R, W, B)
+        add("S", cost, lambda: [S.activation(out, a, fn, bias=bias, scale=scale)], R, W, B)
+
+    def sc(m):
+        return max(64, m) + CFG["SX"]
+
+    def gather(eng, out, win, m, R, W):
+        if eng == "V":
+            vcp(out, win, gc_(m), R, W)
+        else:
+            act(out, win, F.Identity, gc_(m), R, W)
 
     def mms(lst, R, W, B, first=True, last=True):
         def fn():
-            r = []
-            for q, (o, l, x, _) in enumerate(lst):
-                r.append(PE.matmul(o, l, x, first and q == 0, last and q == len(lst) - 1))
-            return r
-        i = add("P", pc(*[y[3] for y in lst]), fn, R, W, B)
+            return [PE.matmul(o, l, x, first and q == 0, last and q == len(lst) - 1) for q, (o, l, x, _) in enumerate(lst)]
+        i = add("P", sum(CFG["PEC"] * max(64, y[3]) for y in lst), fn, R, W, B)
         nodes[i].update(grp=(0 if last else 1) if first else (3 if last else 2))
 
     def mset(ap, v, m, W):
         add("V", vc(m), lambda: [V.memset(ap, v)], (), W)
 
-    def load(q, name, out, cost):
-        eng = {"S": S, "Y": SY}[q]
+    def load(eng, name, out, cost):
         add("net", cost, None, (), (name,), sem=("ld_" + name, 16))
         eng.dma_start(out, T[name][:, :]).then_inc(T.sem["ld_" + name], 16)
-    load("S", "xt", T.tab[:, :], 9000)
-    load("Y", "stk", T.stkI[:, :], 3000)
-    load("Y", "z", T.zl[:, 0:K], 3500)
-    load("Y", "w", T.wI[:, :], 4000)
-    load("Y", "bas", T.basI[:, :], 4500)
-    load("Y", "ln", T.lnI[:, :], 5000)
-    load("Y", "con", T.conI[:, :], 5500)
+    XT = CFG["XT"]
+    load(SY, "stk", T.stkI[:, :], 2500)
+    load(S, "xt", T.tab[:, :], XT)
+    load(SY, "z", T.zl[:, 0:K], XT)
+    load(SY, "w", T.wI[:, :], XT + 200)
+    load(SY, "bas", T.bl[:, 0:K], XT + 600)
+    load(SY, "ln", T.lnI[:, :], XT + 700)
+    load(SY, "con", T.conI[:, :], XT + 1200)
 
-    def iota(out, pat, base, cm, m, W):
-        add("G", 130 + 2 * CY * m, lambda: [g.iota(out, pat, base, cm)], (), W)
-    ib, fb = T.ib, T.fb
-    iota(T.pi[:, 0:1], [[1, 1]], 0, 1, 1, ("pi0",))
-    iota(ib[:, 128:256], [[-16, 8], [0, 16]], 0, 1, 128, ("GM",))
-    iota(ib[:, 256:384], [[0, 8], [1, 16]], 1, 0, 128, ("MI",))
-    iota(ib[:, 0:128], [[-1, 128]], 0, 1, 128, ("FQ",))
-    iota(T.ki[:, :], [[16, 16]], 0, 0, 16, ("ki",))
-    iota(T.E8i[:, :], [[1, 8], [0, 16]], 0, -1, 128, ("E8i",))
+    def iota(out, pat, base, cm, m, W, small=False):
+        if small:
+            add("G", 130 + 2 * m, lambda: [g.iota(out, pat, base, cm, allow_small_or_imprecise_dtypes=True)], (), W)
+        else:
+            add("G", 130 + 2 * m, lambda: [g.iota(out, pat, base, cm)], (), W)
+    pi, pf = T.pi, T.pf
+    iota(pi[:, 0:1], [[1, 1]], 0, 1, 1, ("p",))
+    iota(T.X[:, :], [[1, 144]], 0, 0, 144, ("X",), True)
+    iota(T.Xg[:, :], [[1, 8], [0, 16]], 0, 0, 128, ("Xg",), True)
+    iota(T.Xr[:, :], [[0, 8], [1, 16]], 0, 0, 128, ("Xr",), True)
+    iota(pi[:, 16:32], [[-1, 16]], 16, 1, 16, ("ri",))
+    iota(pi[:, 8:16], [[16, W1]], 0, 0, W1, ("ki",))
+    col = {}
 
-    def cmx(j):
-        return T.cm[:, j * 128:(j + 1) * 128]
-    BD, Ib, nI, U, BDh, BD8, I264, ONE, nUN, I2kb, nI32, I128 = [cmx(j) for j in range(12)]
+    def pcol(name, i0, s1, s2, o1, o2, R):
+        col[name] = pf[:, len(col):len(col) + 1]
+        vts(col[name], i0, s1, s2, o1, o2, vc(1), R, (name,))
+    vts(pi[:, 1:2], pi[:, 0:1], 15, None, A.bitwise_and, None, vc(1), ("p",), ("pr",))
+    vts(pi[:, 2:3], pi[:, 0:1], 4, None, A.arith_shift_right, None, vc(1), ("p",), ("pg",))
+    for j, nm in enumerate(("pp", "r", "g")):
+        col[nm] = pf[:, j:j + 1]
+    vcp(pf[:, 0:3], pi[:, 0:3], vc(1), ("p", "pr", "pg"), ("pp", "r", "g"))
+    r_, g_ = col["r"], col["g"]
+    va, vb = (1.0, 0.0) if CFG["VM"] == "V" else (0.5, 0.5)
+    pcol("g15", g_, 16.0, 15.0, A.mult, A.add, ("g",))
+    pcol("g16", g_, 16.0, None, A.mult, None, ("g",))
+    pcol("is0", r_, 0.5, None, A.is_lt, None, ("r",))
+    pcol("th1", r_, VR + 0.5, -6.5, A.is_lt, A.mult, ("r",))
+    pcol("th2", col["is0"], -90.0, -3.0, A.mult, A.add, ("is0",))
+    pcol("thr", col["th1"], col["th2"], None, A.add, None, ("th1", "th2"))
+    pcol("cut", r_, -1.0 if CFG["HIT"] == "S" else 0.0, 0.0 if CFG["HIT"] == "S" else 1.0, A.mult, A.add, ("r",))
+    pcol("a2", col["is0"], 8192.0, None, A.mult, None, ("is0",))
+    pcol("a1", col["is0"], -8192.0, None, A.mult, None, ("is0",))
+    pcol("bx", r_, 14.5, -16.0 * 8192, A.is_gt, A.mult, ("r",))
+    pcol("by", col["is0"], -8192.0 * (15.5 + 15 * vb), 8192.0, A.mult, A.add, ("is0",))
+    pcol("b2", col["bx"], col["by"], None, A.add, None, ("bx", "by"))
+    pcol("b1", col["is0"], -524288.0 * vb, col["b2"], A.mult, A.subtract, ("is0", "b2"))
+    pcol("n0", r_, 0.5, None, A.is_gt, None, ("r",))
+    pcol("w", T.wI[:, :], 0.0, None, A.add, None, ("w",))
+    mats = {}
 
-    def Sr(r):
-        return T.S[:, r * 128:(r + 1) * 128]
+    def mat(name):
+        mats[name] = T.cm[:, len(mats) * 128:(len(mats) + 1) * 128]
+        return mats[name]
 
-    def Wr(r):
-        return T.Wm[:, r * 128:(r + 1) * 128]
+    def scaled(name, src, f, eng="S"):
+        if eng == "S":
+            act(mat(name), mats[src], F.Copy, sc(128), (src,), (name,), scale=f)
+        else:
+            vts(mat(name), mats[src], f, None, A.mult, None, vc(64), (src,), (name,))
+    Tv, Tq, Tm, Tw = T.Tb, T.Tb, T.Tb, T.Tw
 
-    def Ro(r):
-        return T.Rot[:, r * 128:(r + 1) * 128]
-    I16 = Ro(0)
-    pf = T.pf
-    vts(T.pi[:, 1:2], T.pi[:, 0:1], 15, None, A.bitwise_and, None, vc(1), ("pi0",), ("pi1",))
-    vcp(pf[:, 0:1], T.pi[:, 1:2], vc(1), ("pi1",), ("pc",))
-    vts(pf[:, 1:2], pf[:, 0:1], 8.0, 1.0, A.mult, A.add, vc(1), ("pc",), ("p81",))
-    vts(pf[:, 2:3], pf[:, 0:1], -8.0, 124.0, A.mult, A.add, vc(1), ("pc",), ("p124",))
-    vts(pf[:, 3:4], pf[:, 0:1], VR + 0.5, 6.5, A.is_lt, A.mult, vc(1), ("pc",), ("th1",))
-    vts(pf[:, 4:5], pf[:, 0:1], 0.5, 90.0, A.is_lt, A.mult, vc(1), ("pc",), ("th2",))
-    vtt(pf[:, 5:6], pf[:, 3:4], pf[:, 4:5], A.add, vc(1), ("th1", "th2"), ("th3",))
-    vts(pf[:, 6:7], pf[:, 5:6], -1.0, -3.0, A.mult, A.add, vc(1), ("th3",), ("thr",))
-    vts(pf[:, 10:11], pf[:, 0:1], -1.0, None, A.mult, None, vc(1), ("pc",), ("pneg",))
-    vts(pf[:, 7:8], pf[:, 0:1], 14.5, -128.0, A.is_gt, A.mult, vc(1), ("pc",), ("r15a",))
-    vts(pf[:, 8:9], pf[:, 7:8], 8.0, None, A.add, None, vc(1), ("r15a",), ("r15",))
-    vcp(pf[:, 9:10], T.wI[:, :], vc(1), ("w",), ("wf",))
-    vts(fb[:, 0:128], ib[:, 128:256], 0.0, None, A.is_ge, None, vc(128), ("GM",), ("f0",))
-    vts(fb[:, 128:256], ib[:, 128:256], 15.0, None, A.is_le, None, vc(128), ("GM",), ("f1",))
-    vtt(BD, fb[:, 0:128], fb[:, 128:256], A.mult, vc(256), ("f0", "f1"), ("BD",))
-    vtt(T.kb2 if False else T.GEc0[:, 0:128], ib[:, 256:384], BD, A.mult, vc(256), ("MI", "BD"), ("E1",))
-    vts(ib[:, 384:512], ib[:, 0:128], 15, None, A.bitwise_and, None, vc(128), ("FQ",), ("FA",))
-    vts(fb[:, 256:384], ib[:, 384:512], 1.0, None, A.add, None, vc(128), ("FA",), ("f2",))
-    vtt(T.GEc0[:, 128:256], fb[:, 256:384], BD, A.mult, vc(256), ("f2", "BD"), ("F1",))
-    vts(Ib, T.GEc0[:, 128:256], 1.0, None, A.is_equal, None, vc(64), ("F1",), ("Ib",))
-    def mul(out, i, s, R, W):
-        act(out, i, F.Copy, vc(128), R, W, scale=s)
-    mul(nI, Ib, -1.0, ("Ib",), ("nI",))
+    def pick(buf, j, r):
+        return buf[:, 144 * j + 15 - r:144 * j + 143 - r]
+    vts(mat("I"), T.X[:, 0:128], col["pp"], None, A.is_equal, None, vc(64), ("X", "pp"), ("I",))
+    vts(T.Tb[:, 0:144], T.X[:, :], col["g15"], None, A.is_equal, None, vc(72), ("X", "g15"), ("Tv",))
+    scaled("nI", "I", -1.0)
+    vts(mat("BD"), T.Xg[:, :], g_, None, A.is_equal, None, vc(64), ("Xg", "g"), ("BD",))
+    add("G", 170 + 256, lambda: [g.affine_select(mats["U"], mats["BD"], [[1, 128]], A.is_ge, 0.0, 0, -1)], ("BD",), ("U",))
+    mat("U")
+    act(Tw[:, :], T.Tb[:, 0:144], F.Copy, sc(144), ("Tv", "w"), ("Tw",), scale=col["w"])
+    act(T.Tb[:, 144:288], T.Tb[:, 0:144], F.Copy, sc(144), ("Tv",), ("Tq",), scale=0.25)
+    vts(T.Tb[:, 288:432], T.Tb[:, 0:144], col["n0"], -H * va, A.mult, A.mult, vc(72), ("Tv", "n0"), ("Tm",))
+    scaled("nUN", "I", -4096.0)
+    scaled("n19", "I", -524288.0 * va)
+    scaled("BI", "I", 32768.0)
+    scaled("hI", "I", 0.5)
+    vts(mat("S0"), mats["BD"], col["is0"], None, A.mult, None, vc(64), ("BD", "is0"), ("S0",))
+    scaled("C1", "S0", -4096.0 * va)
+    scaled("C1b", "S0", -4096.0 * vb)
+    scaled("C2", "S0", 32768.0 * va)
+    scaled("C2b", "S0", 2048.0 - 65536.0 + 32768.0 * vb)
+    vts(mat("B2"), mats["BD"], col["n0"], -8192.0 * va, A.mult, A.mult, vc(64), ("BD", "n0"), ("B2",))
+    scaled("B1", "B2", -1.0)
+    for nm in "12":
+        vts(mat("t" + nm), T.Xr[:, :], col["a" + nm], col["b" + nm], A.mult, A.add, vc(64), ("Xr", "a" + nm, "b" + nm), ("t" + nm,))
+        vtt(mat("A" + nm), mats["t" + nm], mats["BD"], A.mult, vc(256), ("t" + nm, "BD"), ("A" + nm,))
+    mset(mat("ONE"), 32.0, 64, ("ONE",))
+    vts(T.E8[:, :], T.Xg[0:8, :], pf[0:8, 0:1], None, A.is_equal, None, vc(64), ("Xg", "pp"), ("E8",))
+    m_ = mats
+    vts(pi[:, 32:48], pi[:, 16:32], 15, None, A.bitwise_and, None, vc(16), ("ri",), ("rj",))
+    vts(pf[:, 32:48], pi[:, 32:48], col["g16"], None, A.add, None, vc(16), ("rj", "g16"), ("rk",))
+
+    def Ro(j, r):
+        return T.Rot[:, (16 * j + r) * 128:(16 * j + r + 1) * 128]
     for r in range(16):
-        vts(Sr(r), T.GEc0[:, 0:128], r + 1.0, None, A.is_equal, None, vc(64), ("E1",), ("S%d" % r,))
-    SALL = tuple("S%d" % r for r in range(16))
-    vts(fb[:, 0:128], ib[:, 0:128], 0.0, None, A.is_le, None, vc(128), ("FQ",), ("f0",))
-    vtt(U, fb[:, 0:128], BD, A.mult, vc(256), ("f0", "BD"), ("U",))
-    for r in range(16):
-        vts(Ro(r), T.GEc0[:, 128:256], r + 1.0, None, A.is_equal, None, vc(64), ("F1",), ("Ro%d" % r,))
-    for h in range(4):
-        act(T.Wm[:, h * 512:(h + 1) * 512], T.S[:, h * 512:(h + 1) * 512], F.Copy, vc(512), SALL + ("wf",), ("Wm%d" % h,), scale=pf[:, 9:10])
-    mul(nUN, Ib, -8192.0, ("Ib",), ("nUN",))
-    mul(I2kb, Ib, 2048.0, ("Ib",), ("I2kb",))
-    mul(nI32, Ib, -32.0, ("Ib",), ("nI32",))
-    mul(I128, Ib, float(n), ("Ib",), ("I128",))
-    mul(BDh, BD, pf[:, 8:9], ("BD", "r15"), ("BDh",))
-    mul(BD8, BD, 8.0, ("BD",), ("BD8",))
-    mul(I264, Ib, float(CD), ("Ib",), ("I264",))
-    mul(T.I2k[:, :], I16, 2048.0, ("Ro0",), ("I2k",))
-    mset(ONE, 1.0, 64, ("ONE",))
-    vts(T.E8[:, :], T.E8i[:, :], 0.0, None, A.is_equal, None, vc(128), ("E8i",), ("E8",))
+        vts(Ro(0, r), T.X[:, 0:128], pf[:, 32 + r:33 + r], None, A.is_equal, None, vc(64), ("X", "rk"), ("Ro%d" % r,))
+    for b in range(4):
+        act(T.Rot[:, 2048 + 512 * b:2560 + 512 * b], T.Rot[:, 512 * b:512 * b + 512], F.Copy, sc(512),
+            tuple("Ro%d" % r for r in range(4 * b, 4 * b + 4)), ("Rp%d" % b,), scale=4096.0)
+    I16 = Ro(0, 0)
     kf, kb = T.kf, T.kb
-    vts(kf[:, 0:16], T.ki[:, :], pf[:, 0:1], None, A.add, None, vc(16), ("ki", "pc"), ("kf",))
-    vts(kf[:, 16:32], kf[:, 0:16], 16.0, None, A.mult, None, vc(16), ("kf",), ("k16",))
-    vcp(kb[:, 0:16], kf[:, 0:16], vc(16), ("kf",), ("kb",))
-    vcp(kb[:, 16:32], kf[:, 16:32], vc(16), ("k16",), ("kb16",))
-    vts(kf[:, 32:48], kf[:, 16:32], 15.5, None, A.add, None, vc(16), ("k16",), ("k16h",))
-    mset(kb[:, 32:48], 16.0, 16, ("kb6",))
-    mset(T.smask[:, :], 1.0, RW // 2, ("smask",))
-    mset(T.smask[:, 0:RW:16], 0.0, n, ("smask",))
-    for t in range(NT):
-        mset(T.cst[:, t * n:(t + 1) * n], 2048.0 + 4096.0 * (t + 1), n, ("cst%d" % t,))
-    mset(T.AW[:, 0:CD], 0.0, CD, ("AW0",))
-    for p in range(2):
-        mset(T["CW%d" % p][:, K:CD], 0.0, 8, ("CZ%d" % p,))
-        mset(T["YW%d" % p][:, K:CD], 0.0, 8, ("YZ%d" % p,))
+    vts(kf[:, 0:W1], pi[:, 8:16], r_, None, A.add, None, vc(8), ("ki", "r"), ("kf",))
+    vts(kb[:, 0:W1], kf[:, 0:W1], 16.0, None, A.mult, None, vc(8), ("kf",), ("kb16",))
+    vts(kf[:, W1:2 * W1], kf[:, 0:W1], 16.0, 15.5, A.mult, A.add, vc(8), ("kf",), ("k16h",))
+    for h in range(2):
+        vcp(kb[:, W1 + h * W1 // 2:W1 + (h + 1) * W1 // 2], kf[:, 0:W1 // 2], vc(8), ("kf",), ("kH%d" % h,))
     for c in range(NC):
-        mset(T["Rc%d" % c][:, RW:RW + 16], 0.0, 16, ("Rz%d" % c,))
-        mset(T["Pc%d" % c][:, RW + 1:RW + 16], 0.0, 16, ("P%d" % c,))
-        mset(T["Pc%d" % c][:, 0:1], 0.0, 16, ("P%d" % c,))
-    mset(T.ac[:, 0:1], 32.0 * 248, 1, ("A32",))
+        vts(T["wfc%d" % c][:, W1:2 * W1], kf[:, 0:W1], 16.0, 16.0 * n * c, A.mult, A.add, vc(8), ("kf",), ("k16_%d" % c,))
+    mset(T.smask[:, :], 1.0, 512, ("smask",))
+    mset(T.smask[:, 0:1024:16], 0.0, 64, ("smask",))
+    for p in range(2):
+        mset(T["CW%d" % p][:, 1:2 * K:2], -4096.0, K, ("CZ%d" % p,))
+    for c in range(NC):
+        mset(T["Rc%d" % c][:, RW:RW + 16], 0.0, 16, ("Rz_%d" % c,))
+        mset(T["Pc%d" % c][:, RW + 1:RW + 16], 0.0, 16, ("Pz_%d" % c,))
+        mset(T["Pc%d" % c][:, 0:1], 0.0, 16, ("Py_%d" % c,))
+    mset(T.ac[:, 0:1], 0.0, 1, ("A0",))
     for c in range(NC):
         vcp(T.stl[:, c * n:(c + 1) * n], T.stkI[:, c * n:(c + 1) * n], vc(n), ("stk",), ("st0_%d" % c,))
-    for c in range(NC):
-        vts(T.bl[:, c * n:(c + 1) * n], T.basI[:, c * n:(c + 1) * n], -2048.0, None, A.add, None, vc(n), ("bas",), ("b0_%d" % c,))
     lo = [0]
 
     def send(dst, o, i, sem, R, W):
@@ -379,225 +378,215 @@ def rank_program(g, core, T, topo):
         def fn():
             g.remote_dma(o, i, T.sem[sem], T.sem.lo, pid, rid, m)
             return []
-        add("G", 1500, fn, R, W)
+        add("G", 1000, fn, R, W)
     for c in range(NC):
-        send(hs[c], T.bl[:, c * n:(c + 1) * n], T.bl[:, c * n:(c + 1) * n], "hb0", ("b0_%d" % c,), ("snt%d" % c,))
+        send(hs[c], T.bl[:, c * n:(c + 1) * n], T.bl[:, c * n:(c + 1) * n], "hb0", ("bas",), ("snt%d" % c,))
     pz = T.pz
     vcp(T.lnB[:, :], T.lnI[:, :], vc(K), ("ln",), ("lnB",))
     mms([(T.pd2[:, 0:K], T.E8[:, :], T.lnB[:, :], K)], ("E8", "lnB"), ("pd2",), ("pd2",))
-    act(T.YW0[:, 0:K], T.pd2[:, 0:K], F.Identity, vc(K), ("pd2",), ("Y0",), ("pd2",), bias=-6.0, scale=8.0)
-    vts(T.lm0[:, :], T.pd2[:, 0:K], pf[:, 0:1], None, A.is_gt, None, vc(K), ("pd2", "pc"), ("lm0",), ("pd2",))
-    vtt(T.CW0[:, 0:K], T.conI[:, :], T.lm0[:, :], A.mult, vc(2 * K), ("con", "lm0"), ("C0",))
-    vcp(pz[:, 256:512], T.conI[:, :], vc(K), ("con",), ("full",), ("pz",))
+    vts(T.pd2[:, 0:K], T.pd2[:, 0:K], r_, -4096.0, A.is_le, A.mult, vc(K), ("pd2", "r"), ("pd2",), ("pd2",))
+    vtt(T.CW0[:, 0:2 * K:2], T.conI[:, :], T.pd2[:, 0:K], A.add, vc(K), ("con", "pd2"), ("C0_0", "C0_1"), ("pd2",))
     for t in range(1, NT):
         for c in range(NC):
-            add("net", LAT * t, None, ("snt%d" % c,), ("b%d_%d" % (t, c),), sem=("b%d_%d" % (t, c), 8))
+            add("net", LAT * t, None, ("snt%d" % c,), ("b%d_%d" % (t, c),), sem=("b%d_%d" % (t, c), far))
 
     rotp = [0]
 
+    def spare():
+        rotp[0] += 1
+        x = "pd%d" % (rotp[0] % 3)
+        return T[x], (x,)
+    tab = T.tab[:, 0:4096]
+
     def chunk(t, c):
         q = "_%d" % c
-        st, z = "st%d_%d" % (t, c), "z%d_%d" % (t, c)
+        st, z, bs = "st%d_%d" % (t, c), "z%d_%d" % (t, c), "b%d_%d" % (t, c)
         if t == 0:
-            z = "z"
+            z, bs = "z", "bas"
         a0 = t * K + c * n
         stA, zA, bA = T.stl[:, a0:a0 + n], T.zl[:, a0:a0 + n], T.bl[:, a0:a0 + n]
-        X = {k: T[k + "c%d" % c] for k in ("R", "P", "GE", "hit", "nf", "AM", "xh", "sb", "rotW", "rg", "pm", "yg", "nmp", "rotK", "baM", "wi", "wf", "wl", "pvb")}
+        R, P, GE, hit, nf, M, y, sb, rotW, rg, ru, vm, bm, low, ef, wi_, wf_, wl_ = [
+            T[x + "c%d" % c] for x in "R P GE hit nf M y sb rotW rg ru vm bm low ef wi wf wl".split()]
         pa, pw = T["pa%d" % c], T["pw%d" % c]
         PA, PW = ("pa%d" % c,), ("pw%d" % c,)
         par = t % 2
-        CW, YW = T["CW%d" % par], T["YW%d" % par]
+        CW = T["CW%d" % par][:, :]
+        CK = ("C%d_0" % par, "C%d_1" % par, "CZ%d" % par)
         k0 = c * n
 
         def k(*xs):
             return tuple(x + q for x in xs)
 
-        def wi(j):
-            return X["wi"][:, j * W1:(j + 1) * W1]
+        def wi(j, m=1):
+            return wi_[:, j * W1:(j + m) * W1]
 
-        def wf(j):
-            return X["wf"][:, j * W1:(j + 1) * W1]
+        def wf(j, m=1):
+            return wf_[:, j * W1:(j + m) * W1]
 
-        def wl(j):
-            return X["wl"][:, j * W1:(j + 1) * W1]
+        def wl(j, m=1):
+            return wl_[:, j * W1:(j + m) * W1]
 
         def pwx(j):
             return pw[:, j * W1:(j + 1) * W1]
         zP = pz[:, k0:k0 + n]
-        mms([(zP, Ib, zA, n)], ("Ib", z), k("zP"), ("pz",))
-        tab = T.tab[:, 0:4096]
-        R = X["R"]
-        RR = ()
-        for qi, (ge, x0, x1) in enumerate(GSPLIT):
-            o, w = R[:, 16 * x0:16 * x1], tab.indirect(T.stl[:, a0 + x0:a0 + x1])
-            if ge == "V":
-                add("V", gc_(16 * (x1 - x0)), lambda o=o, w=w: [V.tensor_copy(o, w)], ("xt", st), k("R%d" % qi))
-            else:
-                act(o, w, F.Identity, gc_(16 * (x1 - x0)), ("xt", st), k("R%d" % qi))
-            RR += k("R%d" % qi)
-        vts(X["sb"][:, :], stA, -2048.0, None, A.add, None, vc(n / 2), (st,), k("sb"))
-        GE = X["GE"]
-        if t == 0 and c == 0:
-            RR0 = RR + tuple("Ro%d" % r for r in range(16)) + SALL
-        GEs = []
-        i0 = VR + 1
-        grp = 0
-        vrow = list(range(1, VR + 1))
-        first = [True]
-        srows = []
-        while i0 < 16:
-            srows.append(list(range(i0, min(16, i0 + 4))))
-            i0 += 4
-        for rows in srows:
-            x = rotp[0] % 3
-            rotp[0] += 1
-            pd = T["pd%d" % x]
+        mms([(zP, m_["I"], zA, n)], ("I", z), k("zP"), ("pz",))
+        RR = []
+        for qi, (ge, x0, x1) in enumerate(CFG["GATHER"]):
+            gather(ge, R[:, 16 * x0:16 * x1], tab.indirect(T.stl[:, a0 + x0:a0 + x1]), 16 * (x1 - x0), ("xt", st), k("R%d" % qi))
+            RR.append((x0, x1, "R%d%s" % (qi, q)))
+        RALL = tuple(x[2] for x in RR)
+        vts(sb[:, :], stA, -2048.0, None, A.add, None, vc(n / 2), (st,), k("sb"))
+        for l0 in range(0, n, SUB):
+            l1 = l0 + SUB
+            RS = tuple(x[2] for x in RR if x[0] < l1 and l0 < x[1])
+            u = "%d" % l0
 
-            def fn(rows=rows, pd=pd):
-                r = []
+            def ge(i, m=1):
+                return GE[:, 16 * l0 + i * SUB:16 * l0 + (i + m) * SUB]
+
+            def row(i):
+                return R[:, 16 * l0 + i:16 * l1:16]
+            parts = []
+            per = 512 // SUB
+            for i0 in range(VR + 1, 16, per):
+                rows = list(range(i0, min(16, i0 + per)))
+                pd, PD = spare()
+                lst = []
                 for jj, i in enumerate(rows):
-                    o = pd[:, jj * n:(jj + 1) * n]
-                    r.append(PE.matmul(o, Ib, R[:, i:RW:16], True, False))
-                    r.append(PE.matmul(o, nI, zA, False, True))
-                return r
-            add("P", pc(*([n] * 2 * len(rows))), fn, RR + ("Ib", "nI", z), ("pd%d" % x,), ("pd%d" % x,))
-            act(GE[:, rows[0] * n:(rows[-1] + 1) * n], pd[:, 0:len(rows) * n], F.Sign, vc(len(rows) * n), ("pd%d" % x,), k("GE%d" % rows[0]) + (("E1", "F1") if t == 0 and c == 0 else ()), ("pd%d" % x,), bias=0.5)
-        for i in vrow:
-            vtt(GE[:, i * n:(i + 1) * n], R[:, i:RW:16], zP, A.is_ge, vc(n), RR + k("zP"), k("GE%d" % i) + (("E1", "F1") if t == 0 and c == 0 else ()), ("pz",))
-        parts = [vrow] + srows
-        vo = pa[:, 0:n]
-        for j, rows in enumerate(parts):
-            keys = k(*["GE%d" % i for i in rows]) if j == 0 else k("GE%d" % rows[0])
-            mms([(vo, Sr(i), GE[:, i * n:(i + 1) * n], n) for i in rows], keys + SALL, k("votes"), PA, j == 0, j == len(parts) - 1)
-        if HV[c]:
-            vts(X["hit"][:, :], vo, pf[:, 6:7], 0.0, A.add, A.is_ge, vc(n), k("votes") + ("thr",), k("hit"), PA)
+                    o = pd[:, jj * SUB:(jj + 1) * SUB]
+                    lst += [(o, m_["I"], row(i), True, False), (o, m_["nI"], T.zl[:, a0 + l0:a0 + l1], False, True)]
+                add("P", CFG["PEC"] * max(64, SUB) * len(lst), lambda lst=lst: [PE.matmul(*x) for x in lst], RS + ("I", "nI", z), PD, PD)
+                act(ge(i0, len(rows)), pd[:, 0:len(rows) * SUB], F.Sign, sc(len(rows) * SUB), PD, k("GE%s_%d" % (u, i0)), PD, bias=0.5)
+                parts.append((rows, k("GE%s_%d" % (u, i0))))
+            for i in range(1, VR + 1):
+                vtt(ge(i), row(i), pz[:, k0 + l0:k0 + l1], A.is_ge, vc(SUB), RS + k("zP"), k("GE%s_%d" % (u, i)), ("pz",))
+            if VR:
+                parts.insert(0, (list(range(1, VR + 1)), k(*["GE%s_%d" % (u, i) for i in range(1, VR + 1)])))
+            for j, (rows, keys) in enumerate(parts):
+                mms([(pa[:, l0:l1], pick(Tv, 0, i), ge(i), SUB) for i in rows], keys + ("Tv",), k("vo" + u), PA, j == 0, j == len(parts) - 1)
+        for l0 in range(0, n, 64):
+            RS = tuple(x[2] for x in RR if x[0] < l0 + 64 and l0 < x[1])
+            s0 = 16 * l0
+            add("V", vc(512), lambda s0=s0: [V.tensor_tensor_scan(P[:, 1 + s0:1025 + s0], T.smask[:, :], R[:, s0:s0 + 1024], 0.0, A.mult, A.max)],
+                RS + ("smask",), k("P%d" % l0))
+        PALL = k(*["P%d" % l0 for l0 in range(0, n, 64)])
+        VO = k(*["vo%d" % l0 for l0 in range(0, n, SUB)])
+        vo, co, L1, L2 = [pa[:, j * n:(j + 1) * n] for j in range(4)]
+        if CFG["HIT"] == "V":
+            vts(hit[:, :], vo, col["thr"], 0.0, A.add, A.is_ge, vc(n), VO + ("thr",), k("hit"), PA)
         else:
-            act(X["hit"][:, :], vo, F.Sign, vc(n), k("votes") + ("thr",), k("hit"), PA, bias=pf[:, 6:7])
-        co = pa[:, n:2 * n]
-        mms([(co, U, X["hit"][:, :], n)], k("hit") + ("U",), k("C"), PA)
-        if HV[c]:
-            vts(X["nf"][:, :], co, 0.5, None, A.is_lt, None, vc(n), k("C"), k("nf"), PA)
+            act(hit[:, :], vo, F.Sign, sc(n), VO + ("thr",), k("hit"), PA, bias=col["thr"])
+        mms([(co, m_["U"], hit[:, :], n)], k("hit") + ("U",), k("C"), PA)
+        if CFG["NF"] == "V":
+            vts(nf[:, :], co, col["cut"], None, A.is_lt, None, vc(n), k("C") + ("cut",), k("nf"), PA)
         else:
-            act(X["nf"][:, :], co, F.Relu, vc(n), k("C") + ("pneg",), k("nf"), PA, bias=pf[:, 10:11], scale=-1.0)
-        for h in range(2):
-            s0, s1 = h * RW // 2, (h + 1) * RW // 2
-            add("V", vc(RW / 4), lambda s0=s0, s1=s1: [V.tensor_tensor_scan(X["P"][:, 1 + s0:1 + s1], T.smask[:, s0:s1], R[:, s0:s1], 0.0, A.mult, A.max)], RR + ("smask",), ("P%d%s" % (c, "ab"[h]),))
-        for b4 in range(16 // RWN):
-            x = rotp[0] % 3
-            rotp[0] += 1
-            pd = T["pd%d" % x]
-
-            def fn(pd=pd, b4=b4):
-                return [PE.matmul(pd[:, jj * n:(jj + 1) * n], Ro(RWN * b4 + jj), X["sb"][:, :], True, True) for jj in range(RWN)]
-            add("P", pc(*([n] * RWN)), fn, k("sb") + tuple("Ro%d" % r for r in range(16)), ("pd%d" % x,), ("pd%d" % x,))
-            act(X["rotW"][:, b4 * RWN * n:(b4 + 1) * RWN * n], pd[:, 0:RWN * n], F.Copy, vc(RWN * n), ("pd%d" % x,), k("rw%d" % b4), ("pd%d" % x,))
-        nf = X["nf"]
-        mms([(pwx(0), Ib, kb[:, 16:16 + W1], W1)] + [(pwx(0), Sr(r), nf[:, r:n:16], W1) for r in range(16)], k("nf") + ("Ib", "kb16") + SALL, k("hw"), PW)
+            act(nf[:, :], co, F.Relu, sc(n), k("C") + ("cut",), k("nf"), PA, bias=col["cut"], scale=-1.0)
+        vtt(R[:, 16:RW + 16:16], zP, P[:, 16:RW + 16:16], A.subtract, vc(n), PALL + k("zP", "Rz"), RALL + k("Rs"), ("pz",))
+        for b in range(16 * H // 512):
+            pd, PD = spare()
+            per = 512 // H
+            lst = []
+            for jj in range(per):
+                o = pd[:, jj * H:(jj + 1) * H]
+                lst += [(o, Ro(0, per * b + jj), sb[:, 0:H], True, False), (o, Ro(1, per * b + jj), sb[:, H:n], False, True)]
+            add("P", CFG["PEC"] * 64 * len(lst), lambda lst=lst: [PE.matmul(*x) for x in lst], k("sb") + tuple("Rp%d" % j for j in range(4)), PD, PD)
+            act(rotW[:, b * 512:(b + 1) * 512], pd[:, :], F.Identity, sc(512), PD, k("rw%d" % b), PD, bias=2048.0 * 4097)
+        mms([(pwx(0), m_["I"], kb[:, 0:W1], W1)] + [(pwx(0), pick(Tv, 0, r), nf[:, r:n:16], W1) for r in range(16)], k("nf") + ("I", "kb16", "Tv"), k("hw"), PW)
         vcp(wl(0), pwx(0), vc(8), k("hw"), k("l1"), PW)
-        vtt(T.unb[:, c * 8:c * 8 + 8], pwx(0), kf[:, 32:32 + W1], A.is_ge, vc(8), k("hw") + ("k16h",), k("unb"), PW)
-        vts(wf(2), pwx(0), 128.0, None, A.mult, None, vc(8), k("hw"), k("h128"), PW)
-        AM = X["AM"]
-        add("V", gc_(n), lambda: [V.tensor_copy(AM[:, n:2 * n], X["P"][:, :].indirect(wl(0)))], k("l1") + ("P%da" % c, "P%db" % c, "P%d" % c), k("M"))
-        act(X["xh"][:, :], R[:, :].indirect(wl(0)), F.Identity, gc_(n), k("l1") + RR + ("Rz%d" % c,), k("xh"))
-        mms([(pwx(1), Ib, kb[:, 32:32 + W1], W1)] + [(pwx(1), Wr(r), AM[:, n + r:2 * n:16], W1) for r in range(16)], k("M") + ("Wm0", "Wm1", "Wm2", "Wm3", "Ib", "kb6"), k("uw"), PW)
-        mms([(pwx(2), Sr(r), X["xh"][:, r:n:16], W1) for r in range(16)] + [(pwx(2), nUN, T.unb[:, c * 8:c * 8 + 8], W1)], k("xh", "unb") + SALL + ("nUN",), k("vw"), PW)
-        uv = X["wi"][:, 4 * W1:6 * W1]
-        vts(uv, pw[:, W1:3 * W1], 0.0, None, A.max, None, vc(16), k("uw", "vw"), k("ui"), PW)
-        vts(wi(1), wi(4), 4095, None, A.bitwise_and, None, vc(8), k("ui"), k("uc"))
-        vtt(wi(2), wi(1), wi(1), A.mult, vc(8), k("uc"), k("uq"))
-        vts(wi(3), wi(2), T.ac[:, 0:1], None, A.add, None, vc(8), k("uq") + ("A32",), k("ur"))
-        vts(wi(0), wi(3), 5, 255, A.arith_shift_right, A.bitwise_and, vc(8), k("ur"), k("uj"))
-        vts(wi(6), wi(5), 3, None, A.bitwise_and, None, vc(8), k("ui"), k("v3"))
-        vts(X["pvb"][:, :], wi(6), 1.0, None, A.min, None, vc(8), k("v3"), k("pvb"))
-        vts(wf(3), X["pvb"][:, :], -256.0, 256.0, A.mult, A.add, vc(8), k("pvb"), k("np"))
-        vtt(wi(7), wi(0), wf(3), A.max, vc(8), k("uj", "np"), k("um"))
-        vcp(wl(1), wi(7), vc(8), k("um"), k("lj"))
-        act(X["yg"][:, :], YW[:, 0:CD].indirect(wl(1)), F.Identity, gc_(n), k("lj") + ("Y%d" % par, "YZ%d" % par), k("yg"))
-        act(X["pm"][:, :], CW[:, 0:CD].indirect(wl(1)), F.Identity, gc_(n), k("lj") + ("C%d" % par, "CZ%d" % par), k("pm"), bias=-2048.0)
-        mms([(pwx(3), I2kb, kb[:, 0:W1], W1), (pwx(3), nI, kb[:, 0:W1], W1), (pwx(3), nI32, X["pvb"][:, :], W1)] + [(pwx(3), Sr(r), X["yg"][:, r:n:16], W1) for r in range(16)],
-            k("yg", "pvb") + SALL + ("I2kb", "nI", "nI32", "kb"), k("mw"), PW)
-        vtt(wi(8), wf(2), pwx(3), A.subtract, vc(8), k("h128", "mw"), k("x1"), PW)
-        vts(wi(9), wi(8), RW - 1, None, A.bitwise_and, None, vc(8), k("x1"), k("x2"))
-        vcp(wl(2), wi(9), vc(8), k("x2"), k("lr"))
-        act(X["rg"][:, :], X["rotW"][:, :].indirect(wl(2)), F.Identity, gc_(n), k("lr", *["rw%d" % b for b in range(16 // RWN)]), k("rg"))
-        hy = pa[:, 2 * n:3 * n]
-        mms([(hy, BDh, nf[:, :], n), (hy, nI, X["yg"][:, :], n)], k("nf", "yg") + ("BDh", "nI"), k("hy"), PA)
-        vts(X["nmp"][:, :], X["yg"][:, :], pf[:, 1:2], None, A.is_lt, None, vc(n / 2), k("yg") + ("p81",), k("nmp"))
-        vts(hy, hy, pf[:, 2:3], None, A.is_ge, None, vc(n), k("hy") + ("p124",), k("hy"), PA)
-        vtt(vo, X["nmp"][:, :], hy, A.subtract, vc(n), k("nmp", "hy"), k("votes"), PA)
-        vtt(X["baM"][:, :], bA, hy, A.mult, vc(n), k("hy") + ("b%d_%d" % (t, c),), k("baM"), PA)
-        no = pa[:, 3 * n:4 * n]
-        mms([(no, I16, X["pm"][:, :], n), (no, T.I2k[:, :], X["nmp"][:, :], n), (no, I16, X["baM"][:, :], n)], k("pm", "nmp", "baM") + ("Ro0", "I2k"), k("new"), PA, True, False)
-        vtt(X["rotK"][:, :], X["rg"][:, :], vo, A.mult, vc(n), k("rg", "votes"), k("rotK"), PA)
-        mms([(no, I16, X["rotK"][:, :], n)], k("rotK") + ("Ro0",), k("new"), PA, False, True)
-        if t < NT - 1:
-            so = T.sto[:, a0:a0 + n]
-            vts(so, no, 2048.0, None, A.add, None, vc(n), k("new"), k("so"), PA)
-            send(hs[0], T.stl[:, a0 + K:a0 + K + n], so, "hs%d_%d" % (t + 1, c), k("so"), ("xs%d_%d" % (t, c),))
-            add("net", LAT, None, ("xs%d_%d" % (t, c),), ("st%d_%d" % (t + 1, c),), sem=("s%d_%d" % (t + 1, c), 8))
+        gather(CFG["M"], M[:, :], P[:, :].indirect(wl(0)), n, k("l1", "Pz", "Py") + PALL, k("M"))
+        gather(CFG["Y"], y[:, :], R[:, :].indirect(wl(0)), n, k("l1", "Rs") + RALL, k("y"))
+        unb = T.unb[:, c * W1:(c + 1) * W1]
+        vtt(unb, pwx(0), kf[:, W1:2 * W1], A.is_ge, vc(8), k("hw") + ("k16h",), k("unb"), PW)
+        if CFG["H64"] == "V":
+            vts(wf(2), pwx(0), float(H), H * (16 - 15 * vb), A.mult, A.add, vc(8), k("hw"), k("h64"), PW)
         else:
-            vts(T.stf[:, k0:k0 + n], no, 2048.0, None, A.add, None, vc(n), k("new"), k("so"), PA)
-        mms([(pwx(4), Ib, kb[:, 0:W1], W1), (pwx(4), I128, T.unb[:, c * 8:c * 8 + 8], W1)], k("unb") + ("Ib", "kb", "I128"), k("mk"), PW)
-        vcp(wl(3), pwx(4), vc(8), k("mk"), k("lm"), PW)
-        mms([(co, Ib, X["xh"][:, :], n), (co, nI, zA, n)], k("xh") + ("Ib", "nI", z), k("C"), PA)
-        act(AM[:, 0:n], co, F.Abs, vc(n), k("C"), k("ad"), PA)
+            act(wf(2), pwx(0), F.Identity, sc(8), k("hw"), k("h64"), PW, scale=float(H), bias=H * (16 - 15 * vb))
+        mms([(pwx(1), pick(Tw, 0, r), M[:, r:n:16], W1) for r in range(16)], k("M") + ("Tw",), k("uw"), PW)
+        pv = pz[:, 272 + c * W1:272 + (c + 1) * W1]
+        mms([(pv, pick(Tq, 1, r), y[:, r:n:16], W1) for r in range(16)] + [(pv, m_["nUN"], unb, W1)], k("y", "unb") + ("Tq", "nUN"), k("vw"), ("pz",))
+        vts(wi(0), pwx(1), 16.0, None, A.add, None, vc(8), k("uw"), k("ui"), PW)
+        vts(wi(1), wi(0), 4095, None, A.bitwise_and, None, vc(8), k("ui"), k("uc"))
+        vtt(wi(2), wi(1), wi(1), A.mult, vc(8), k("uc"), k("uq"))
+        vts(wi(3), wi(2), -65792.0, T.ac[:, t:t + 1], A.add, A.add, vc(8), k("uq") + ("A%d" % t,), k("ur"))
+        vts(wi(4), wi(3), 4, 510, A.arith_shift_right, A.bitwise_and, vc(8), k("ur"), k("uj"))
+        vts(wi(6), pv, -0.4, 0.0, A.add, A.max, vc(8), k("vw"), k("vr"), ("pz",))
+        vtt(wf(0), wi(6), pv, A.is_ge, vc(8), k("vr", "vw"), k("np"), ("pz",))
+        m = 1
+        if t < NT - 1:
+            m = 2
+            vts(wi(5), wi(0), 15, None, A.bitwise_and, None, vc(8), k("ui"), k("t1"))
+        vtt(wi(8, m), wi(4, m), wf(0, m), A.add, vc(8), k("uj", "np", "k16") + (k("t1") if m == 2 else ()), k("um"))
+        vcp(wl(1, m), wi(8, m), vc(8), k("um"), k("lj"))
+        CJ = CW.indirect(wl(1))
+        if CFG["VM"] == "V":
+            vts(vm[:, :], CJ, 0.0, None, A.is_ge, None, gc_(n), k("lj") + CK, k("vm"))
+        else:
+            act(vm[:, :], CJ, F.Sign, gc_(n), k("lj") + CK, k("vm"), bias=0.5)
+        mms([(L2, m_["A2"], nf[:, :], n), (L2, m_["B2"], vm[:, :], n)], k("nf", "vm") + ("A2", "B2"), k("L2"), PA)
+        mms([(pwx(3), m_["I"], kb[:, W1:2 * W1], W1)] + [(pwx(3), pick(Tm, 2, r), vm[:, r:n:16], W1) for r in range(16)],
+            k("vm") + ("I", "kH0", "kH1", "Tm"), k("mw"), PW)
+        mms([(L1, m_["A1"], nf[:, :], n), (L1, m_["B1"], vm[:, :], n), (L1, m_["n19"], vm[:, :], n)], k("nf", "vm") + ("A1", "B1", "n19"), k("L1"), PA)
+        vtt(bm[:, :], bA, L2, A.min, vc(n), k("L2") + (bs,), k("bm"), PA)
+        vtt(low[:, :], CJ, bm[:, :], A.max, gc_(n), k("lj", "bm") + CK, k("low"))
+        vtt(wi(10), wf(2), pwx(3), A.add, vc(8), k("h64", "mw"), k("x1"), PW)
+        vts(wi(11), wi(10), 16 * H - 1, None, A.bitwise_and, None, vc(8), k("x1"), k("x2"))
+        vcp(wl(3), wi(11), vc(8), k("x2"), k("lr"))
+        vcp(rg[:, :], rotW[:, :].indirect(wl(3)), gc_(n), k("lr", *["rw%d" % b for b in range(16 * H // 512)]), k("rg"))
+        vts(ru[:, 0:H], rg[:, 0:H], 4095, None, A.bitwise_and, None, vc(H), k("rg"), k("ru0"))
+        vts(ru[:, H:n], rg[:, H:n], 12, None, A.arith_shift_right, None, vc(H), k("rg"), k("ru1"))
+        vtt(L1, ru[:, :], L1, A.min, vc(n), k("ru0", "ru1", "L1"), k("L1"), PA)
+        if t < NT - 1:
+            vtt(ef[:, :], low[:, :], L1, A.max, vc(n), k("low", "L1"), k("ef"), PA)
+            so = T.sto[:, a0:a0 + n]
+            vcp(so, ef[:, :], vc(n), k("ef"), k("so"))
+            send(hs[0], T.stl[:, a0 + K:a0 + K + n], so, "hs%d_%d" % (t + 1, c), k("so"), ("xs%d_%d" % (t, c),))
+            add("net", LAT, None, ("xs%d_%d" % (t, c),), ("st%d_%d" % (t + 1, c),), sem=("s%d_%d" % (t + 1, c), far))
+        else:
+            vtt(T.stf[:, k0:k0 + n], low[:, :], L1, A.max, vc(n), k("low", "L1"), k("so"), PA)
+        mms([(co, m_["I"], y[:, :], n), (co, m_["nI"], zA, n)], k("y") + ("I", "nI", z), k("C"), PA)
         zo = T.zo[:, a0:a0 + n]
-        act(zo, AM[:, :].indirect(wl(3)), F.Identity, gc_(n), k("lm", "ad", "M"), k("zo"))
+        act(zo, co, F.Abs, sc(n), k("C"), k("zo"), PA)
         if t < NT - 1:
             send(hs[1], T.zl[:, a0 + K:a0 + K + n], zo, "hz%d_%d" % (t + 1, c), k("zo"), ("xz%d_%d" % (t, c),))
-            add("net", LAT, None, ("xz%d_%d" % (t, c),), ("z%d_%d" % (t + 1, c),), sem=("z%d_%d" % (t + 1, c), 8))
+            add("net", LAT, None, ("xz%d_%d" % (t, c),), ("z%d_%d" % (t + 1, c),), sem=("z%d_%d" % (t + 1, c), far))
 
     def tail(t):
         par = t % 2
-        CW, YW, CN, YN = T["CW%d" % par], T["YW%d" % par], T["CW%d" % (1 - par)], T["YW%d" % (1 - par)]
         for c in range(NC):
             q = "_%d" % c
-            X = {k: T[k + "c%d" % c] for k in ("nf", "AM", "sb", "wi", "wl", "pvb", "told", "tnew")}
-            pa, pw = T["pa%d" % c], T["pw%d" % c]
+            nf, M, sb, vm, wl_, told, thf, tnew, cd = [T[x + "c%d" % c] for x in "nf M sb vm wl told thf tnew cd".split()]
+            pw = T["pw%d" % c]
             PW = ("pw%d" % c,)
             k0 = c * n
 
             def k(*xs):
                 return tuple(x + q for x in xs)
             if t < NT - 1:
-                wi1 = X["wi"][:, 4 * W1:5 * W1]
-                w11, w12 = X["wi"][:, 11 * W1:12 * W1], X["wi"][:, 12 * W1:13 * W1]
-                la = X["wl"][:, 4 * W1:5 * W1]
-                vts(w11, wi1, 15, None, A.bitwise_and, None, vc(8), k("ui"), k("t1"))
-                vtt(w12, w11, kf[:, 16 + c * W1:16 + (c + 1) * W1], A.add, vc(8), k("t1") + ("k16",), k("t2"))
-                vcp(la, w12, vc(8), k("t2"), k("la"))
-                add("V", gc_(n), lambda X=X, la=la: [V.tensor_tensor(X["told"][:, :], T.tab[:, 0:4096].indirect(la), X["AM"][:, n:2 * n], A.add)], k("la", "M") + ("xt",), k("told"))
-                vts(X["tnew"][:, :], X["told"][:, :], 1, None, A.arith_shift_right, None, vc(n), k("told"), k("tnew"))
-                add("V", 60 + 3.8 * CY * n, lambda X=X, la=la: [V.tensor_copy(T.tab[:, 0:4096].indirect(la), X["tnew"][:, :])], k("la", "tnew"), ("xt",))
-            sl = T.pw0[:, 80 + c * W1:80 + (c + 1) * W1]
-            mms([(sl, Ib, kb[:, c * W1:(c + 1) * W1], W1), (sl, I264, X["pvb"][:, :], W1)], k("pvb") + ("Ib", "I264", "kb"), k("sl"), ("pw0",))
-            SS, hB = pw[:, 128:256], pw[:, 256:384]
-            mms([(SS, I16, X["sb"][:, :], n), (SS, I16, T.cst[:, t * n:(t + 1) * n], n)], k("sb") + ("Ro0", "cst%d" % t), k("SS"), PW)
-            mms([(hB, BD8, X["nf"][:, :], n)], k("nf") + ("BD8",), k("hB"), PW)
-            aw = T.AW[:, CD + k0:CD + k0 + n]
-            vtt(aw, X["nf"][:, :], SS, A.mult, vc(n), k("nf", "SS"), k("aw"), PW)
-            if t < NT - 1:
-                act(CW[:, CD + k0:CD + k0 + n], aw, F.Relu, vc(n), k("aw"), k("cc"), (), bias=-4096.0 * (t + 1))
-            act(YW[:, CD + k0:CD + k0 + n], hB, F.Identity, vc(n), k("hB"), k("yc"), PW, bias=-6.0)
-        sel = T.sel[:, :]
-        SEL = ("sel",)
-        vcp(sel, T.pw0[:, 80:80 + K // 16], vc(16), ("sl_0", "sl_1"), SEL, ("pw0",))
-        act(YN[:, 0:K], YW[:, :].indirect(sel), F.Identity, gc_(K), SEL + ("Y%d" % par, "YZ%d" % par, "yc_0", "yc_1"), ("Y%d" % (1 - par),))
+                TA = tab.indirect(wl_[:, 2 * W1:3 * W1])
+                if CFG["TOLD"] == "V":
+                    vtt(told[:, :], TA, M[:, :], A.add, gc_(n), k("lj", "M") + ("xt",), k("told"))
+                    vts(tnew[:, :], told[:, :], 1, None, A.arith_shift_right, None, vc(n), k("told"), k("tnew"))
+                else:
+                    hm = pw[:, n:2 * n]
+                    mms([(hm, m_["hI"], M[:, :], n)], k("M") + ("hI",), k("hm"), PW)
+                    act(thf[:, :], TA, F.Identity, gc_(n), k("lj") + ("xt",), k("thf"), bias=-0.25, scale=0.5)
+                    vtt(tnew[:, :], thf[:, :], hm, A.add, vc(n), k("thf", "hm"), k("tnew"), PW)
+                vcp(TA, tnew[:, :], 55 + 3.8 * n, k("lj", "tnew"), ("xt",))
+            P1, P2 = pw[:, 2 * n:3 * n], pw[:, 3 * n:4 * n]
+            mms([(P1, m_["C1"], vm[:, :], n)] + ([(P1, m_["C1b"], nf[:, :], n)] if vb else []), k("vm", "nf") + ("C1", "C1b"), k("P1"), PW)
+            mms([(P2, I16, sb[:, :], n), (P2, m_["BI"], nf[:, :], n), (P2, m_["C2b"], nf[:, :], n), (P2, m_["C2"], vm[:, :], n)],
+                k("sb", "nf", "vm") + ("Ro0", "BI", "C2", "C2b"), k("P2"), PW)
+            vtt(cd[:, :], T["CW%d" % par][:, 2 * k0:2 * (k0 + n):2], P1, A.add, vc(n), k("P1", "C%d" % par), k("cd"), PW)
+            o = T["CW%d" % (1 - par)][:, 2 * k0:2 * (k0 + n):2] if t < NT - 1 else T.yci[:, k0:k0 + n]
+            vtt(o, cd[:, :], P2, A.max, vc(n), k("cd", "P2"), k("C%d" % (1 - par)), PW)
         if t < NT - 1:
-            act(CN[:, 0:K], CW[:, :].indirect(sel), F.Identity, gc_(K), SEL + ("C%d" % par, "CZ%d" % par, "cc_0", "cc_1"), ("C%d" % (1 - par),))
-        act(T.asel[:, :], T.AW[:, :].indirect(sel), F.Identity, gc_(K), SEL + ("AW0", "aw_0", "aw_1"), ("asel",))
-        vtt(pz[:, 256:512], T.asel[:, :], pz[:, 256:512], A.max, vc(K), ("asel", "full"), ("full",), ("pz",))
-        if t < NT - 1:
-            to = T.pw0[:, 64:80]
-            mms([(to, ONE, T.unb[:, :], 16)], ("unb_0", "unb_1", "ONE"), ("tot",), ("pw0",))
-            add("V", vc(16), lambda: [V.tensor_reduce(T.ac[:, 1:2], to, AxisListType.X, A.add)], ("tot",), ("ac1",), ("pw0",))
-            vts(T.ai[:, 0:1], T.ac[:, 1:2], 248.0, None, A.add, None, vc(1), ("ac1",), ("ai0",))
-            vts(T.ai[:, 1:2], T.ai[:, 0:1], 255, None, A.bitwise_and, None, vc(1), ("ai0",), ("ai1",))
-            vts(T.ac[:, 0:1], T.ai[:, 1:2], 32.0, None, A.mult, None, vc(1), ("ai1",), ("A32",))
+            to = pz[:, 256:272]
+            mms([(to, m_["ONE"], T.unb[:, :], 16)], ("unb_0", "unb_1", "ONE"), ("tot",), ("pz",))
+            add("V", vc(16), lambda: [V.tensor_reduce(T.ac[:, t + 1:t + 2], to, AxisListType.X, A.add)], ("tot",), ("A%d" % (t + 1),), ("pz",))
 
     for t in range(NT):
         for c in range(NC):
-            BON[0] = BONUS * (1 - c)
+            BON[0] = CFG["BONUS"] * (1 - c)
             chunk(t, c)
         BON[0] = 0.0
         tail(t)
@@ -608,26 +597,20 @@ def rank_program(g, core, T, topo):
             SY.dma_start(out, i).then_inc(T.sem.outs, 16)
             return []
         outs[0] += 16
-        add("Y", 100, fn, R, ())
+        add("Y", 2000, fn, R, ())
     store(T.yz[:, :], T.zo[:, (NT - 1) * K:NT * K], ("zo_0", "zo_1"))
     store(T.ys[:, :], T.stf[:, :], ("so_0", "so_1"))
-    yo = T.pa0[0:8, 0:K]
-    mms([(yo, T.S[:, 0:128:16], T["YW%d" % (NT % 2)][:, 0:K], K)], SALL + ("Y%d" % (NT % 2), "votes_0", "C_0"), ("yo", "votes_0", "C_0"), ("pa0",))
-    vts(T.ynf[:, :], yo, 96.0, 1.0 / 128, A.add, A.mult, vc(K), ("yo",), ("ynf",), ("pa0",))
+    last = ("C%d_0" % (NT % 2), "C%d_1" % (NT % 2))
+    vts(T.ycv[:, :], T.yci[:, :], 0.0, None, A.is_ge, None, vc(K), last, ("ycv",))
+    pd, PD = spare()
+    mms([(pd[0:8, 0:K], T.Tb[:, 15:143:16], T.ycv[:, :], K)], ("Tv", "ycv"), PD, PD)
+    act(T.ynf[:, :], pd[0:8, 0:K], F.Copy, sc(K), PD, ("ynf",), PD)
     store(T.yn[:, :], T.ynf[:, :], ("ynf",))
-    vcp(T.yci[:, :], pz[:, 256:512], vc(K), ("full",), ("yci",), ("pz",))
-    vts(T.ycj[:, :], T.yci[:, :], 4095, None, A.bitwise_and, None, vc(K), ("yci",), ("ycj",))
+    vts(T.ycj[:, :], T.yci[:, :], 4095, None, A.bitwise_and, None, vc(K), last, ("ycj",))
     vcp(T.ycf[:, :], T.ycj[:, :], vc(K), ("ycj",), ("ycf",))
     store(T.yc[:, :], T.ycf[:, :], ("ycf",))
 
     if "o" not in ORDERS:
-        seen_kn = {}
-        for x in nodes:
-            seen_kn[x["kn"]] = seen_kn.get(x["kn"], 0) + 1
-        names = sorted(q for q, m in seen_kn.items() if m >= 4 and q[0] in "VSPG")
-        for x in nodes:
-            if BTS and x["kn"] in names:
-                x["bonus"] += 800.0 * (LEV.index(BTS[names.index(x["kn"])]) - 32)
         ORDERS["o"] = schedule(nodes)
     order, extra, _ = ORDERS["o"]
     Q = {"V": V, "S": S, "P": PE, "G": g, "Y": SY}
@@ -640,9 +623,6 @@ def rank_program(g, core, T, topo):
         if x["sem"]:
             done[i] = [x["sem"]]
             continue
-        if x["fn"] is None:
-            done[i] = []
-            continue
         e = x["eng"]
         need = {}
         for d in tuple(x["deps"]) + extra[i]:
@@ -653,9 +633,9 @@ def rank_program(g, core, T, topo):
                 Q[e].wait_ge(T.sem[s], v)
                 seen[e][s] = v
         r = x["fn"]()
-        for ins in r:
+        if r:
             cnt[e] += 1
-            ins.then_inc(T.sem[SM[e]], 1)
+            r[-1].then_inc(T.sem[SM[e]], 1)
         done[i] = [(SM[e], cnt[e])] if r else []
     SY.wait_ge(T.sem.outs, outs[0])
     for e in cnt:

from concourse.mybir import AluOpType as A, AxisListType, ActivationFunctionType as F

NT = 5
K = 256
NC = 2
n = K // NC
H = n // 2
W1 = n // 16
RW = 16 * n
CFG = dict(
    VR=7,
    SUB=64,
    GATHER=(("V", 0, 32), ("S", 32, 64), ("S", 64, 128)),
    HIT="S", NF="S", M="V", Y="S", VM="V", TOLD="S", H64="V",
    LAT=4000, PEC=0.5, SX=80, WS=45, WK=100, BONUS=3000.0, SLK=60, XT=6000,
)

SCRATCH = {
    "tab": ("sbuf", [128, 4096], "bfloat16"),
    "stl": ("sbuf", [128, NT * K], "uint16"), "sto": ("sbuf", [128, NT * K], "uint16"),
    "zl": ("sbuf", [128, NT * K], "bfloat16"), "zo": ("sbuf", [128, NT * K], "bfloat16"),
    "bl": ("sbuf", [128, NT * K], "int32"),
    "stkI": ("sbuf", [128, K], "int32"), "conI": ("sbuf", [128, K], "int32"),
    "lnI": ("sbuf", [8, K], "int32"), "lnB": ("sbuf", [8, K], "bfloat16"), "wI": ("sbuf", [128, 1], "int32"),
    "stf": ("sbuf", [128, K], "float32"),
    "X": ("sbuf", [128, 144], "bfloat16"), "Xg": ("sbuf", [128, 128], "bfloat16"), "Xr": ("sbuf", [128, 128], "bfloat16"),
    "Tb": ("sbuf", [128, 3 * 144], "bfloat16"), "Tw": ("sbuf", [128, 144], "float16"),
    "Rot": ("sbuf", [128, 2 * 16 * 128], "float16"),
    "cm": ("sbuf", [128, 20 * 128], "bfloat16"),
    "E8": ("sbuf", [8, 128], "bfloat16"),
    "pi": ("sbuf", [128, 64], "int32"), "pf": ("sbuf", [128, 48], "float32"),
    "kf": ("sbuf", [128, 16], "float32"), "kb": ("sbuf", [128, 16], "bfloat16"),
    "smask": ("sbuf", [128, 1024], "bfloat16"),
    "CW0": ("sbuf", [128, 2 * K], "float32"), "CW1": ("sbuf", [128, 2 * K], "float32"),
    "unb": ("sbuf", [128, 16], "bfloat16"), "ac": ("sbuf", [128, 8], "float32"),
    "yci": ("sbuf", [128, K], "int32"), "ycj": ("sbuf", [128, K], "int32"), "ycf": ("sbuf", [128, K], "float32"),
    "ycv": ("sbuf", [128, K], "bfloat16"), "ynf": ("sbuf", [8, K], "float32"),
    "pz": ("psum", [128, 512], "float32"),
}
for _c in range(NC):
    for _nm, _w, _d in (("R", RW + 16, "bfloat16"), ("P", RW + 16, "bfloat16"), ("GE", RW, "bfloat16"),
                        ("hit", n, "bfloat16"), ("nf", n, "bfloat16"), ("M", n, "bfloat16"), ("y", n, "bfloat16"),
                        ("sb", n, "float16"), ("rotW", 16 * H, "float32"), ("rg", n, "int32"), ("ru", n, "int32"),
                        ("vm", n, "bfloat16"), ("bm", n, "float32"), ("low", n, "float32"), ("ef", n, "float32"),
                        ("wi", 16 * W1, "int32"), ("wf", 4 * W1, "float32"), ("wl", 4 * W1, "uint16"),
                        ("told", n, "int32"), ("thf", n, "float32"), ("tnew", n, "int32"), ("cd", n, "float32")):
        SCRATCH[_nm + "c%d" % _c] = ("sbuf", [128, _w], _d)
    SCRATCH["pa%d" % _c] = ("psum", [128, 512], "float32")
    SCRATCH["pw%d" % _c] = ("psum", [128, 512], "float32")
for _x in range(3):
    SCRATCH["pd%d" % _x] = ("psum", [128, 512], "float32")

LOADS = ["xt", "stk", "z", "w", "ln", "con", "bas"]
SEMAPHORES = (["sV", "sS", "sP", "sG", "lo", "outs"] + ["ld_" + x for x in LOADS]
              + ["%s%d_%d" % (p, t, c) for p in ("s", "z", "b") for t in range(1, NT) for c in range(NC)]
              + ["h%s%d_%d" % (p, t, c) for p in ("s", "z") for t in range(1, NT) for c in range(NC)]
              + ["hb%d" % t for t in range(NT)])


def vc(m, f=1.0):
    return max(64, m * f) + 15


def gc_(m):
    return 55 + 1.56 * m


ORDERS = {}


def schedule(nodes):
    N = len(nodes)
    succ = [[] for _ in range(N)]
    for i, x in enumerate(nodes):
        for d in x["deps"]:
            succ[d].append(i)
    pri = [0.0] * N
    for i in range(N - 1, -1, -1):
        pri[i] = nodes[i]["cost"] + 60 + max([pri[j] for j in succ[i]] + [0.0])
    for i in range(N):
        pri[i] += nodes[i]["bonus"]
    left = [len(x["deps"]) for x in nodes]
    ready = {}
    est = [0.0] * N
    for i in range(N):
        if left[i] == 0:
            ready.setdefault(nodes[i]["eng"], set()).add(i)
    free = {}
    opened = set()
    bank = {}
    order, extra = [], [()] * N
    end = [0.0] * N
    while len(order) < N:
        best = None
        for e, rs in ready.items():
            f = free.get(e, 0.0)
            c = []
            for i in rs:
                if e == "P" and nodes[i]["grp"] < 2 and opened & set(nodes[i]["banks"]):
                    continue
                s = max(est[i], f if e != "net" else 0.0)
                for b in nodes[i]["banks"]:
                    lb = bank.get(b)
                    if lb and nodes[lb]["eng"] != e:
                        s = max(s, end[lb] + CFG["WK"])
                c.append((s, i))
            if not c:
                continue
            m = min(c)[0]
            k = max((pri[i], -s, i) for s, i in c if s <= m + CFG["SLK"])
            if best is None or m < best[0]:
                best = (m, k[2], -k[1])
        i, s = best[1], best[2]
        x = nodes[i]
        e = x["eng"]
        ready[e].discard(i)
        end[i] = s + x["cost"]
        free[e] = end[i]
        ex = []
        for b in x["banks"]:
            lb = bank.get(b)
            if lb is not None and nodes[lb]["eng"] != e:
                ex.append(lb)
            bank[b] = i
        extra[i] = tuple(ex)
        if x["grp"] == 1:
            opened.update(x["banks"])
        elif x["grp"] == 3:
            opened.difference_update(x["banks"])
        order.append(i)
        for j in succ[i]:
            left[j] -= 1
            est[j] = max(est[j], end[i] + (CFG["WK"] if nodes[j]["eng"] != e else CFG["WS"]))
            if left[j] == 0:
                ready.setdefault(nodes[j]["eng"], set()).add(j)
    return order, extra, max(end)


def helpers(core, nxt, topo):
    cs = [c for c in topo.cores_of(core) if c != core and topo.may_write(c, nxt)]
    same = [c for c in cs if topo.die(c) == topo.die(core)]
    other = [c for c in cs if topo.die(c) != topo.die(core)]
    return [same[0], other[0]]


def hand_on(g, core, T, topo, rank, which):
    cores = T.cores
    me = cores[rank]
    nr = (rank + 1) % len(cores)
    nxt = cores[nr]
    nh = helpers(nxt, cores[(nr + 1) % len(cores)], topo)[which]
    lo = [0]

    def send(dst, o, i, sem):
        rid, pid = topo.addr(dst, core)
        m = topo.mask(core, nxt)
        g.remote_dma(o, i, T.sem[sem], T.sem.lo, pid, rid, m)
        lo[0] += len(topo.engines(core, nxt))

    def base(t):
        a = t * K + which * n
        b = T.bl[:, a:a + n]
        g.wait_ge(T.sem["hb%d" % t], len(topo.engines(me, core) if t == 0 else topo.engines(core, nxt)))
        if t < NT - 1:
            send(nh, T.bl[:, a + K:a + K + n], b, "hb%d" % (t + 1))
        if t > 0:
            send(me, b, b, "b%d_%d" % (t, which))
    p, buf = (("s", T.stl), ("z", T.zl))[which]
    base(0)
    for t in range(1, NT):
        base(t)
        for c in range(NC):
            a = t * K + c * n
            g.wait_ge(T.sem["h%s%d_%d" % (p, t, c)], len(topo.engines(me, core)))
            send(nxt, buf[:, a:a + n], buf[:, a:a + n], "%s%d_%d" % (p, t, c))
    g.wait_ge(T.sem.lo, lo[0])


def rank_program(g, core, T, topo):
    cores = T.cores
    NR = len(cores)
    rank = T.rank_of(core)
    if rank is None:
        for r in range(NR):
            if core in topo.cores_of(cores[r]):
                hs = helpers(cores[r], cores[(r + 1) % NR], topo)
                if core in hs:
                    hand_on(g, core, T, topo, r, hs.index(core))
        return
    hs = helpers(core, cores[(rank + 1) % NR], topo)
    far = len(topo.engines(hs[0], cores[(rank + 1) % NR]))
    V, S, PE, SY = g.vector, g.scalar, g.tensor, g.sync
    VR, SUB, LAT = CFG["VR"], CFG["SUB"], CFG["LAT"]
    BON = [0.0]
    nodes = []
    lastw, readers = {}, {}

    def add(eng, cost, fn, R=(), W=(), B=(), sem=None):
        i = len(nodes)
        deps = set()
        for r in R:
            deps.add(lastw[r])
        for w in W:
            if w in lastw:
                deps.add(lastw[w])
            deps.update(readers.get(w, ()))
        deps.discard(i)
        for r in R:
            readers.setdefault(r, []).append(i)
        for w in W:
            lastw[w] = i
            readers[w] = []
        nodes.append(dict(eng=eng, cost=cost, fn=fn, deps=sorted(deps), banks=tuple(B), sem=sem, bonus=BON[0], grp=0))
        return i

    def vts(out, i0, s1, s2, o1, o2, cost, R, W, B=()):
        if o2 is None:
            add("V", cost, lambda: [V.tensor_scalar(out, i0, s1, None, o1)], R, W, B)
        else:
            add("V", cost, lambda: [V.tensor_scalar(out, i0, s1, s2, o1, o2)], R, W, B)

    def vtt(out, a, b, op, cost, R, W, B=()):
        add("V", cost, lambda: [V.tensor_tensor(out, a, b, op)], R, W, B)

    def vcp(out, a, cost, R, W, B=()):
        add("V", cost, lambda: [V.tensor_copy(out, a)], R, W, B)

    def act(out, a, fn, cost, R, W, B=(), bias=0.0, scale=1.0):
        add("S", cost, lambda: [S.activation(out, a, fn, bias=bias, scale=scale)], R, W, B)

    def sc(m):
        return max(64, m) + CFG["SX"]

    def gather(eng, out, win, m, R, W):
        if eng == "V":
            vcp(out, win, gc_(m), R, W)
        else:
            act(out, win, F.Identity, gc_(m), R, W)

    def mms(lst, R, W, B, first=True, last=True):
        def fn():
            return [PE.matmul(o, l, x, first and q == 0, last and q == len(lst) - 1) for q, (o, l, x, _) in enumerate(lst)]
        i = add("P", sum(CFG["PEC"] * max(64, y[3]) for y in lst), fn, R, W, B)
        nodes[i].update(grp=(0 if last else 1) if first else (3 if last else 2))

    def mset(ap, v, m, W):
        add("V", vc(m), lambda: [V.memset(ap, v)], (), W)

    def load(eng, name, out, cost):
        add("net", cost, None, (), (name,), sem=("ld_" + name, 16))
        eng.dma_start(out, T[name][:, :]).then_inc(T.sem["ld_" + name], 16)
    XT = CFG["XT"]
    load(SY, "stk", T.stkI[:, :], 2500)
    load(S, "xt", T.tab[:, :], XT)
    load(SY, "z", T.zl[:, 0:K], XT)
    load(SY, "w", T.wI[:, :], XT + 200)
    load(SY, "bas", T.bl[:, 0:K], XT + 600)
    load(SY, "ln", T.lnI[:, :], XT + 700)
    load(SY, "con", T.conI[:, :], XT + 1200)

    def iota(out, pat, base, cm, m, W, small=False):
        if small:
            add("G", 130 + 2 * m, lambda: [g.iota(out, pat, base, cm, allow_small_or_imprecise_dtypes=True)], (), W)
        else:
            add("G", 130 + 2 * m, lambda: [g.iota(out, pat, base, cm)], (), W)
    pi, pf = T.pi, T.pf
    iota(pi[:, 0:1], [[1, 1]], 0, 1, 1, ("p",))
    iota(T.X[:, :], [[1, 144]], 0, 0, 144, ("X",), True)
    iota(T.Xg[:, :], [[1, 8], [0, 16]], 0, 0, 128, ("Xg",), True)
    iota(T.Xr[:, :], [[0, 8], [1, 16]], 0, 0, 128, ("Xr",), True)
    iota(pi[:, 16:32], [[-1, 16]], 16, 1, 16, ("ri",))
    iota(pi[:, 8:16], [[16, W1]], 0, 0, W1, ("ki",))
    col = {}

    def pcol(name, i0, s1, s2, o1, o2, R):
        col[name] = pf[:, len(col):len(col) + 1]
        vts(col[name], i0, s1, s2, o1, o2, vc(1), R, (name,))
    vts(pi[:, 1:2], pi[:, 0:1], 15, None, A.bitwise_and, None, vc(1), ("p",), ("pr",))
    vts(pi[:, 2:3], pi[:, 0:1], 4, None, A.arith_shift_right, None, vc(1), ("p",), ("pg",))
    for j, nm in enumerate(("pp", "r", "g")):
        col[nm] = pf[:, j:j + 1]
    vcp(pf[:, 0:3], pi[:, 0:3], vc(1), ("p", "pr", "pg"), ("pp", "r", "g"))
    r_, g_ = col["r"], col["g"]
    va, vb = (1.0, 0.0) if CFG["VM"] == "V" else (0.5, 0.5)
    pcol("g15", g_, 16.0, 15.0, A.mult, A.add, ("g",))
    pcol("g16", g_, 16.0, None, A.mult, None, ("g",))
    pcol("is0", r_, 0.5, None, A.is_lt, None, ("r",))
    pcol("th1", r_, VR + 0.5, -6.5, A.is_lt, A.mult, ("r",))
    pcol("th2", col["is0"], -90.0, -3.0, A.mult, A.add, ("is0",))
    pcol("thr", col["th1"], col["th2"], None, A.add, None, ("th1", "th2"))
    pcol("cut", r_, -1.0 if CFG["HIT"] == "S" else 0.0, 0.0 if CFG["HIT"] == "S" else 1.0, A.mult, A.add, ("r",))
    pcol("a2", col["is0"], 8192.0, None, A.mult, None, ("is0",))
    pcol("a1", col["is0"], -8192.0, None, A.mult, None, ("is0",))
    pcol("bx", r_, 14.5, -16.0 * 8192, A.is_gt, A.mult, ("r",))
    pcol("by", col["is0"], -8192.0 * (15.5 + 15 * vb), 8192.0, A.mult, A.add, ("is0",))
    pcol("b2", col["bx"], col["by"], None, A.add, None, ("bx", "by"))
    pcol("b1", col["is0"], -524288.0 * vb, col["b2"], A.mult, A.subtract, ("is0", "b2"))
    pcol("n0", r_, 0.5, None, A.is_gt, None, ("r",))
    pcol("w", T.wI[:, :], 0.0, None, A.add, None, ("w",))
    mats = {}

    def mat(name):
        mats[name] = T.cm[:, len(mats) * 128:(len(mats) + 1) * 128]
        return mats[name]

    def scaled(name, src, f, eng="S"):
        if eng == "S":
            act(mat(name), mats[src], F.Copy, sc(128), (src,), (name,), scale=f)
        else:
            vts(mat(name), mats[src], f, None, A.mult, None, vc(64), (src,), (name,))
    Tv, Tq, Tm, Tw = T.Tb, T.Tb, T.Tb, T.Tw

    def pick(buf, j, r):
        return buf[:, 144 * j + 15 - r:144 * j + 143 - r]
    vts(mat("I"), T.X[:, 0:128], col["pp"], None, A.is_equal, None, vc(64), ("X", "pp"), ("I",))
    vts(T.Tb[:, 0:144], T.X[:, :], col["g15"], None, A.is_equal, None, vc(72), ("X", "g15"), ("Tv",))
    scaled("nI", "I", -1.0)
    vts(mat("BD"), T.Xg[:, :], g_, None, A.is_equal, None, vc(64), ("Xg", "g"), ("BD",))
    add("G", 170 + 256, lambda: [g.affine_select(mats["U"], mats["BD"], [[1, 128]], A.is_ge, 0.0, 0, -1)], ("BD",), ("U",))
    mat("U")
    act(Tw[:, :], T.Tb[:, 0:144], F.Copy, sc(144), ("Tv", "w"), ("Tw",), scale=col["w"])
    act(T.Tb[:, 144:288], T.Tb[:, 0:144], F.Copy, sc(144), ("Tv",), ("Tq",), scale=0.25)
    vts(T.Tb[:, 288:432], T.Tb[:, 0:144], col["n0"], -H * va, A.mult, A.mult, vc(72), ("Tv", "n0"), ("Tm",))
    scaled("nUN", "I", -4096.0)
    scaled("n19", "I", -524288.0 * va)
    scaled("BI", "I", 32768.0)
    scaled("hI", "I", 0.5)
    vts(mat("S0"), mats["BD"], col["is0"], None, A.mult, None, vc(64), ("BD", "is0"), ("S0",))
    scaled("C1", "S0", -4096.0 * va)
    scaled("C1b", "S0", -4096.0 * vb)
    scaled("C2", "S0", 32768.0 * va)
    scaled("C2b", "S0", 2048.0 - 65536.0 + 32768.0 * vb)
    vts(mat("B2"), mats["BD"], col["n0"], -8192.0 * va, A.mult, A.mult, vc(64), ("BD", "n0"), ("B2",))
    scaled("B1", "B2", -1.0)
    for nm in "12":
        vts(mat("t" + nm), T.Xr[:, :], col["a" + nm], col["b" + nm], A.mult, A.add, vc(64), ("Xr", "a" + nm, "b" + nm), ("t" + nm,))
        vtt(mat("A" + nm), mats["t" + nm], mats["BD"], A.mult, vc(256), ("t" + nm, "BD"), ("A" + nm,))
    mset(mat("ONE"), 32.0, 64, ("ONE",))
    vts(T.E8[:, :], T.Xg[0:8, :], pf[0:8, 0:1], None, A.is_equal, None, vc(64), ("Xg", "pp"), ("E8",))
    m_ = mats
    vts(pi[:, 32:48], pi[:, 16:32], 15, None, A.bitwise_and, None, vc(16), ("ri",), ("rj",))
    vts(pf[:, 32:48], pi[:, 32:48], col["g16"], None, A.add, None, vc(16), ("rj", "g16"), ("rk",))

    def Ro(j, r):
        return T.Rot[:, (16 * j + r) * 128:(16 * j + r + 1) * 128]
    for r in range(16):
        vts(Ro(0, r), T.X[:, 0:128], pf[:, 32 + r:33 + r], None, A.is_equal, None, vc(64), ("X", "rk"), ("Ro%d" % r,))
    for b in range(4):
        act(T.Rot[:, 2048 + 512 * b:2560 + 512 * b], T.Rot[:, 512 * b:512 * b + 512], F.Copy, sc(512),
            tuple("Ro%d" % r for r in range(4 * b, 4 * b + 4)), ("Rp%d" % b,), scale=4096.0)
    I16 = Ro(0, 0)
    kf, kb = T.kf, T.kb
    vts(kf[:, 0:W1], pi[:, 8:16], r_, None, A.add, None, vc(8), ("ki", "r"), ("kf",))
    vts(kb[:, 0:W1], kf[:, 0:W1], 16.0, None, A.mult, None, vc(8), ("kf",), ("kb16",))
    vts(kf[:, W1:2 * W1], kf[:, 0:W1], 16.0, 15.5, A.mult, A.add, vc(8), ("kf",), ("k16h",))
    for h in range(2):
        vcp(kb[:, W1 + h * W1 // 2:W1 + (h + 1) * W1 // 2], kf[:, 0:W1 // 2], vc(8), ("kf",), ("kH%d" % h,))
    for c in range(NC):
        vts(T["wfc%d" % c][:, W1:2 * W1], kf[:, 0:W1], 16.0, 16.0 * n * c, A.mult, A.add, vc(8), ("kf",), ("k16_%d" % c,))
    mset(T.smask[:, :], 1.0, 512, ("smask",))
    mset(T.smask[:, 0:1024:16], 0.0, 64, ("smask",))
    for p in range(2):
        mset(T["CW%d" % p][:, 1:2 * K:2], -4096.0, K, ("CZ%d" % p,))
    for c in range(NC):
        mset(T["Rc%d" % c][:, RW:RW + 16], 0.0, 16, ("Rz_%d" % c,))
        mset(T["Pc%d" % c][:, RW + 1:RW + 16], 0.0, 16, ("Pz_%d" % c,))
        mset(T["Pc%d" % c][:, 0:1], 0.0, 16, ("Py_%d" % c,))
    mset(T.ac[:, 0:1], 0.0, 1, ("A0",))
    for c in range(NC):
        vcp(T.stl[:, c * n:(c + 1) * n], T.stkI[:, c * n:(c + 1) * n], vc(n), ("stk",), ("st0_%d" % c,))
    lo = [0]

    def send(dst, o, i, sem, R, W):
        rid, pid = topo.addr(dst, core)
        m = topo.mask(core, dst)
        lo[0] += len(topo.engines(core, dst))

        def fn():
            g.remote_dma(o, i, T.sem[sem], T.sem.lo, pid, rid, m)
            return []
        add("G", 1000, fn, R, W)
    for c in range(NC):
        send(hs[c], T.bl[:, c * n:(c + 1) * n], T.bl[:, c * n:(c + 1) * n], "hb0", ("bas",), ("snt%d" % c,))
    pz = T.pz
    vcp(T.lnB[:, :], T.lnI[:, :], vc(K), ("ln",), ("lnB",))
    mms([(T.pd2[:, 0:K], T.E8[:, :], T.lnB[:, :], K)], ("E8", "lnB"), ("pd2",), ("pd2",))
    vts(T.pd2[:, 0:K], T.pd2[:, 0:K], r_, -4096.0, A.is_le, A.mult, vc(K), ("pd2", "r"), ("pd2",), ("pd2",))
    vtt(T.CW0[:, 0:2 * K:2], T.conI[:, :], T.pd2[:, 0:K], A.add, vc(K), ("con", "pd2"), ("C0_0", "C0_1"), ("pd2",))
    for t in range(1, NT):
        for c in range(NC):
            add("net", LAT * t, None, ("snt%d" % c,), ("b%d_%d" % (t, c),), sem=("b%d_%d" % (t, c), far))

    rotp = [0]

    def spare():
        rotp[0] += 1
        x = "pd%d" % (rotp[0] % 3)
        return T[x], (x,)
    tab = T.tab[:, 0:4096]

    def chunk(t, c):
        q = "_%d" % c
        st, z, bs = "st%d_%d" % (t, c), "z%d_%d" % (t, c), "b%d_%d" % (t, c)
        if t == 0:
            z, bs = "z", "bas"
        a0 = t * K + c * n
        stA, zA, bA = T.stl[:, a0:a0 + n], T.zl[:, a0:a0 + n], T.bl[:, a0:a0 + n]
        R, P, GE, hit, nf, M, y, sb, rotW, rg, ru, vm, bm, low, ef, wi_, wf_, wl_ = [
            T[x + "c%d" % c] for x in "R P GE hit nf M y sb rotW rg ru vm bm low ef wi wf wl".split()]
        pa, pw = T["pa%d" % c], T["pw%d" % c]
        PA, PW = ("pa%d" % c,), ("pw%d" % c,)
        par = t % 2
        CW = T["CW%d" % par][:, :]
        CK = ("C%d_0" % par, "C%d_1" % par, "CZ%d" % par)
        k0 = c * n

        def k(*xs):
            return tuple(x + q for x in xs)

        def wi(j, m=1):
            return wi_[:, j * W1:(j + m) * W1]

        def wf(j, m=1):
            return wf_[:, j * W1:(j + m) * W1]

        def wl(j, m=1):
            return wl_[:, j * W1:(j + m) * W1]

        def pwx(j):
            return pw[:, j * W1:(j + 1) * W1]
        zP = pz[:, k0:k0 + n]
        mms([(zP, m_["I"], zA, n)], ("I", z), k("zP"), ("pz",))
        RR = []
        for qi, (ge, x0, x1) in enumerate(CFG["GATHER"]):
            gather(ge, R[:, 16 * x0:16 * x1], tab.indirect(T.stl[:, a0 + x0:a0 + x1]), 16 * (x1 - x0), ("xt", st), k("R%d" % qi))
            RR.append((x0, x1, "R%d%s" % (qi, q)))
        RALL = tuple(x[2] for x in RR)
        vts(sb[:, :], stA, -2048.0, None, A.add, None, vc(n / 2), (st,), k("sb"))
        for l0 in range(0, n, SUB):
            l1 = l0 + SUB
            RS = tuple(x[2] for x in RR if x[0] < l1 and l0 < x[1])
            u = "%d" % l0

            def ge(i, m=1):
                return GE[:, 16 * l0 + i * SUB:16 * l0 + (i + m) * SUB]

            def row(i):
                return R[:, 16 * l0 + i:16 * l1:16]
            parts = []
            per = 512 // SUB
            for i0 in range(VR + 1, 16, per):
                rows = list(range(i0, min(16, i0 + per)))
                pd, PD = spare()
                lst = []
                for jj, i in enumerate(rows):
                    o = pd[:, jj * SUB:(jj + 1) * SUB]
                    lst += [(o, m_["I"], row(i), True, False), (o, m_["nI"], T.zl[:, a0 + l0:a0 + l1], False, True)]
                add("P", CFG["PEC"] * max(64, SUB) * len(lst), lambda lst=lst: [PE.matmul(*x) for x in lst], RS + ("I", "nI", z), PD, PD)
                act(ge(i0, len(rows)), pd[:, 0:len(rows) * SUB], F.Sign, sc(len(rows) * SUB), PD, k("GE%s_%d" % (u, i0)), PD, bias=0.5)
                parts.append((rows, k("GE%s_%d" % (u, i0))))
            for i in range(1, VR + 1):
                vtt(ge(i), row(i), pz[:, k0 + l0:k0 + l1], A.is_ge, vc(SUB), RS + k("zP"), k("GE%s_%d" % (u, i)), ("pz",))
            if VR:
                parts.insert(0, (list(range(1, VR + 1)), k(*["GE%s_%d" % (u, i) for i in range(1, VR + 1)])))
            for j, (rows, keys) in enumerate(parts):
                mms([(pa[:, l0:l1], pick(Tv, 0, i), ge(i), SUB) for i in rows], keys + ("Tv",), k("vo" + u), PA, j == 0, j == len(parts) - 1)
        for l0 in range(0, n, 64):
            RS = tuple(x[2] for x in RR if x[0] < l0 + 64 and l0 < x[1])
            s0 = 16 * l0
            add("V", vc(512), lambda s0=s0: [V.tensor_tensor_scan(P[:, 1 + s0:1025 + s0], T.smask[:, :], R[:, s0:s0 + 1024], 0.0, A.mult, A.max)],
                RS + ("smask",), k("P%d" % l0))
        PALL = k(*["P%d" % l0 for l0 in range(0, n, 64)])
        VO = k(*["vo%d" % l0 for l0 in range(0, n, SUB)])
        vo, co, L1, L2 = [pa[:, j * n:(j + 1) * n] for j in range(4)]
        if CFG["HIT"] == "V":
            vts(hit[:, :], vo, col["thr"], 0.0, A.add, A.is_ge, vc(n), VO + ("thr",), k("hit"), PA)
        else:
            act(hit[:, :], vo, F.Sign, sc(n), VO + ("thr",), k("hit"), PA, bias=col["thr"])
        mms([(co, m_["U"], hit[:, :], n)], k("hit") + ("U",), k("C"), PA)
        if CFG["NF"] == "V":
            vts(nf[:, :], co, col["cut"], None, A.is_lt, None, vc(n), k("C") + ("cut",), k("nf"), PA)
        else:
            act(nf[:, :], co, F.Relu, sc(n), k("C") + ("cut",), k("nf"), PA, bias=col["cut"], scale=-1.0)
        vtt(R[:, 16:RW + 16:16], zP, P[:, 16:RW + 16:16], A.subtract, vc(n), PALL + k("zP", "Rz"), RALL + k("Rs"), ("pz",))
        for b in range(16 * H // 512):
            pd, PD = spare()
            per = 512 // H
            lst = []
            for jj in range(per):
                o = pd[:, jj * H:(jj + 1) * H]
                lst += [(o, Ro(0, per * b + jj), sb[:, 0:H], True, False), (o, Ro(1, per * b + jj), sb[:, H:n], False, True)]
            add("P", CFG["PEC"] * 64 * len(lst), lambda lst=lst: [PE.matmul(*x) for x in lst], k("sb") + tuple("Rp%d" % j for j in range(4)), PD, PD)
            act(rotW[:, b * 512:(b + 1) * 512], pd[:, :], F.Identity, sc(512), PD, k("rw%d" % b), PD, bias=2048.0 * 4097)
        mms([(pwx(0), m_["I"], kb[:, 0:W1], W1)] + [(pwx(0), pick(Tv, 0, r), nf[:, r:n:16], W1) for r in range(16)], k("nf") + ("I", "kb16", "Tv"), k("hw"), PW)
        vcp(wl(0), pwx(0), vc(8), k("hw"), k("l1"), PW)
        gather(CFG["M"], M[:, :], P[:, :].indirect(wl(0)), n, k("l1", "Pz", "Py") + PALL, k("M"))
        gather(CFG["Y"], y[:, :], R[:, :].indirect(wl(0)), n, k("l1", "Rs") + RALL, k("y"))
        unb = T.unb[:, c * W1:(c + 1) * W1]
        vtt(unb, pwx(0), kf[:, W1:2 * W1], A.is_ge, vc(8), k("hw") + ("k16h",), k("unb"), PW)
        if CFG["H64"] == "V":
            vts(wf(2), pwx(0), float(H), H * (16 - 15 * vb), A.mult, A.add, vc(8), k("hw"), k("h64"), PW)
        else:
            act(wf(2), pwx(0), F.Identity, sc(8), k("hw"), k("h64"), PW, scale=float(H), bias=H * (16 - 15 * vb))
        mms([(pwx(1), pick(Tw, 0, r), M[:, r:n:16], W1) for r in range(16)], k("M") + ("Tw",), k("uw"), PW)
        pv = pz[:, 272 + c * W1:272 + (c + 1) * W1]
        mms([(pv, pick(Tq, 1, r), y[:, r:n:16], W1) for r in range(16)] + [(pv, m_["nUN"], unb, W1)], k("y", "unb") + ("Tq", "nUN"), k("vw"), ("pz",))
        vts(wi(0), pwx(1), 16.0, None, A.add, None, vc(8), k("uw"), k("ui"), PW)
        vts(wi(1), wi(0), 4095, None, A.bitwise_and, None, vc(8), k("ui"), k("uc"))
        vtt(wi(2), wi(1), wi(1), A.mult, vc(8), k("uc"), k("uq"))
        vts(wi(3), wi(2), -65792.0, T.ac[:, t:t + 1], A.add, A.add, vc(8), k("uq") + ("A%d" % t,), k("ur"))
        vts(wi(4), wi(3), 4, 510, A.arith_shift_right, A.bitwise_and, vc(8), k("ur"), k("uj"))
        vts(wi(6), pv, -0.4, 0.0, A.add, A.max, vc(8), k("vw"), k("vr"), ("pz",))
        vtt(wf(0), wi(6), pv, A.is_ge, vc(8), k("vr", "vw"), k("np"), ("pz",))
        m = 1
        if t < NT - 1:
            m = 2
            vts(wi(5), wi(0), 15, None, A.bitwise_and, None, vc(8), k("ui"), k("t1"))
        vtt(wi(8, m), wi(4, m), wf(0, m), A.add, vc(8), k("uj", "np", "k16") + (k("t1") if m == 2 else ()), k("um"))
        vcp(wl(1, m), wi(8, m), vc(8), k("um"), k("lj"))
        CJ = CW.indirect(wl(1))
        if CFG["VM"] == "V":
            vts(vm[:, :], CJ, 0.0, None, A.is_ge, None, gc_(n), k("lj") + CK, k("vm"))
        else:
            act(vm[:, :], CJ, F.Sign, gc_(n), k("lj") + CK, k("vm"), bias=0.5)
        mms([(L2, m_["A2"], nf[:, :], n), (L2, m_["B2"], vm[:, :], n)], k("nf", "vm") + ("A2", "B2"), k("L2"), PA)
        mms([(pwx(3), m_["I"], kb[:, W1:2 * W1], W1)] + [(pwx(3), pick(Tm, 2, r), vm[:, r:n:16], W1) for r in range(16)],
            k("vm") + ("I", "kH0", "kH1", "Tm"), k("mw"), PW)
        mms([(L1, m_["A1"], nf[:, :], n), (L1, m_["B1"], vm[:, :], n), (L1, m_["n19"], vm[:, :], n)], k("nf", "vm") + ("A1", "B1", "n19"), k("L1"), PA)
        vtt(bm[:, :], bA, L2, A.min, vc(n), k("L2") + (bs,), k("bm"), PA)
        vtt(low[:, :], CJ, bm[:, :], A.max, gc_(n), k("lj", "bm") + CK, k("low"))
        vtt(wi(10), wf(2), pwx(3), A.add, vc(8), k("h64", "mw"), k("x1"), PW)
        vts(wi(11), wi(10), 16 * H - 1, None, A.bitwise_and, None, vc(8), k("x1"), k("x2"))
        vcp(wl(3), wi(11), vc(8), k("x2"), k("lr"))
        vcp(rg[:, :], rotW[:, :].indirect(wl(3)), gc_(n), k("lr", *["rw%d" % b for b in range(16 * H // 512)]), k("rg"))
        vts(ru[:, 0:H], rg[:, 0:H], 4095, None, A.bitwise_and, None, vc(H), k("rg"), k("ru0"))
        vts(ru[:, H:n], rg[:, H:n], 12, None, A.arith_shift_right, None, vc(H), k("rg"), k("ru1"))
        vtt(L1, ru[:, :], L1, A.min, vc(n), k("ru0", "ru1", "L1"), k("L1"), PA)
        if t < NT - 1:
            vtt(ef[:, :], low[:, :], L1, A.max, vc(n), k("low", "L1"), k("ef"), PA)
            so = T.sto[:, a0:a0 + n]
            vcp(so, ef[:, :], vc(n), k("ef"), k("so"))
            send(hs[0], T.stl[:, a0 + K:a0 + K + n], so, "hs%d_%d" % (t + 1, c), k("so"), ("xs%d_%d" % (t, c),))
            add("net", LAT, None, ("xs%d_%d" % (t, c),), ("st%d_%d" % (t + 1, c),), sem=("s%d_%d" % (t + 1, c), far))
        else:
            vtt(T.stf[:, k0:k0 + n], low[:, :], L1, A.max, vc(n), k("low", "L1"), k("so"), PA)
        mms([(co, m_["I"], y[:, :], n), (co, m_["nI"], zA, n)], k("y") + ("I", "nI", z), k("C"), PA)
        zo = T.zo[:, a0:a0 + n]
        act(zo, co, F.Abs, sc(n), k("C"), k("zo"), PA)
        if t < NT - 1:
            send(hs[1], T.zl[:, a0 + K:a0 + K + n], zo, "hz%d_%d" % (t + 1, c), k("zo"), ("xz%d_%d" % (t, c),))
            add("net", LAT, None, ("xz%d_%d" % (t, c),), ("z%d_%d" % (t + 1, c),), sem=("z%d_%d" % (t + 1, c), far))

    def tail(t):
        par = t % 2
        for c in range(NC):
            q = "_%d" % c
            nf, M, sb, vm, wl_, told, thf, tnew, cd = [T[x + "c%d" % c] for x in "nf M sb vm wl told thf tnew cd".split()]
            pw = T["pw%d" % c]
            PW = ("pw%d" % c,)
            k0 = c * n

            def k(*xs):
                return tuple(x + q for x in xs)
            if t < NT - 1:
                TA = tab.indirect(wl_[:, 2 * W1:3 * W1])
                if CFG["TOLD"] == "V":
                    vtt(told[:, :], TA, M[:, :], A.add, gc_(n), k("lj", "M") + ("xt",), k("told"))
                    vts(tnew[:, :], told[:, :], 1, None, A.arith_shift_right, None, vc(n), k("told"), k("tnew"))
                else:
                    hm = pw[:, n:2 * n]
                    mms([(hm, m_["hI"], M[:, :], n)], k("M") + ("hI",), k("hm"), PW)
                    act(thf[:, :], TA, F.Identity, gc_(n), k("lj") + ("xt",), k("thf"), bias=-0.25, scale=0.5)
                    vtt(tnew[:, :], thf[:, :], hm, A.add, vc(n), k("thf", "hm"), k("tnew"), PW)
                vcp(TA, tnew[:, :], 55 + 3.8 * n, k("lj", "tnew"), ("xt",))
            P1, P2 = pw[:, 2 * n:3 * n], pw[:, 3 * n:4 * n]
            mms([(P1, m_["C1"], vm[:, :], n)] + ([(P1, m_["C1b"], nf[:, :], n)] if vb else []), k("vm", "nf") + ("C1", "C1b"), k("P1"), PW)
            mms([(P2, I16, sb[:, :], n), (P2, m_["BI"], nf[:, :], n), (P2, m_["C2b"], nf[:, :], n), (P2, m_["C2"], vm[:, :], n)],
                k("sb", "nf", "vm") + ("Ro0", "BI", "C2", "C2b"), k("P2"), PW)
            vtt(cd[:, :], T["CW%d" % par][:, 2 * k0:2 * (k0 + n):2], P1, A.add, vc(n), k("P1", "C%d" % par), k("cd"), PW)
            o = T["CW%d" % (1 - par)][:, 2 * k0:2 * (k0 + n):2] if t < NT - 1 else T.yci[:, k0:k0 + n]
            vtt(o, cd[:, :], P2, A.max, vc(n), k("cd", "P2"), k("C%d" % (1 - par)), PW)
        if t < NT - 1:
            to = pz[:, 256:272]
            mms([(to, m_["ONE"], T.unb[:, :], 16)], ("unb_0", "unb_1", "ONE"), ("tot",), ("pz",))
            add("V", vc(16), lambda: [V.tensor_reduce(T.ac[:, t + 1:t + 2], to, AxisListType.X, A.add)], ("tot",), ("A%d" % (t + 1),), ("pz",))

    for t in range(NT):
        for c in range(NC):
            BON[0] = CFG["BONUS"] * (1 - c)
            chunk(t, c)
        BON[0] = 0.0
        tail(t)
    outs = [0]

    def store(out, i, R):
        def fn():
            SY.dma_start(out, i).then_inc(T.sem.outs, 16)
            return []
        outs[0] += 16
        add("Y", 2000, fn, R, ())
    store(T.yz[:, :], T.zo[:, (NT - 1) * K:NT * K], ("zo_0", "zo_1"))
    store(T.ys[:, :], T.stf[:, :], ("so_0", "so_1"))
    last = ("C%d_0" % (NT % 2), "C%d_1" % (NT % 2))
    vts(T.ycv[:, :], T.yci[:, :], 0.0, None, A.is_ge, None, vc(K), last, ("ycv",))
    pd, PD = spare()
    mms([(pd[0:8, 0:K], T.Tb[:, 15:143:16], T.ycv[:, :], K)], ("Tv", "ycv"), PD, PD)
    act(T.ynf[:, :], pd[0:8, 0:K], F.Copy, sc(K), PD, ("ynf",), PD)
    store(T.yn[:, :], T.ynf[:, :], ("ynf",))
    vts(T.ycj[:, :], T.yci[:, :], 4095, None, A.bitwise_and, None, vc(K), last, ("ycj",))
    vcp(T.ycf[:, :], T.ycj[:, :], vc(K), ("ycj",), ("ycf",))
    store(T.yc[:, :], T.ycf[:, :], ("ycf",))

    if "o" not in ORDERS:
        ORDERS["o"] = schedule(nodes)
    order, extra, _ = ORDERS["o"]
    Q = {"V": V, "S": S, "P": PE, "G": g, "Y": SY}
    SM = {"V": "sV", "S": "sS", "P": "sP", "G": "sG"}
    cnt = {"V": 0, "S": 0, "P": 0, "G": 0}
    done = {}
    seen = {e: {} for e in Q}
    for i in order:
        x = nodes[i]
        if x["sem"]:
            done[i] = [x["sem"]]
            continue
        e = x["eng"]
        need = {}
        for d in tuple(x["deps"]) + extra[i]:
            for s, v in done[d]:
                need[s] = max(need.get(s, 0), v)
        for s, v in sorted(need.items()):
            if seen[e].get(s, 0) < v:
                Q[e].wait_ge(T.sem[s], v)
                seen[e][s] = v
        r = x["fn"]()
        if r:
            cnt[e] += 1
            r[-1].then_inc(T.sem[SM[e]], 1)
        done[i] = [(SM[e], cnt[e])] if r else []
    SY.wait_ge(T.sem.outs, outs[0])
    for e in cnt:
        g.wait_ge(T.sem[SM[e]], cnt[e])
    g.wait_ge(T.sem.lo, lo[0])
